import numpy as np, ml_dtypes
CORES = [5,29,101,125,133,157,229,253]
N = 8
import mx_ref
BF = ml_dtypes.bfloat16
def gcols(t, e):
    v = np.concatenate([t.reshape(8, 16, -1, 4), np.zeros((8, 16, 1, 4), BF)], axis=2)
    return np.ascontiguousarray(np.stack([v[g][:, e[g]] for g in range(8)])).reshape(128, -1)
def tile(rs):
    return np.stack(rs, axis=2).reshape(128, -1).astype(BF)
def cut(t, i, w=512):
    return t[:, w * i:w * i + w]
def pick(q, e):
    c = np.concatenate([q[0].reshape(128, -1, 4), np.zeros((128, 1, 4), np.uint8)], axis=1); s = np.concatenate([q[1], np.ones((16, 1), np.uint8)], axis=1)
    return (np.ascontiguousarray(c[:, e].reshape(128, -1)), np.ascontiguousarray(s[:, e]))
def join(*qs):
    return (np.concatenate([q[0] for q in qs], axis=1), np.concatenate([q[1] for q in qs], axis=1))
def put(q, e, v):
    c, s = q[0].reshape(128, -1, 4).copy(), q[1].copy(); c[:, e] = v[0].reshape(128, -1, 4); s[:, e] = v[1]
    return (c.reshape(128, -1), s)
def pk(c, s):
    return (np.ascontiguousarray(c), mx_ref.live(s))
def emit(q):
    return q[0], q[1]
def packed(v, rng):
    q = [mx_ref.quantize(np.ascontiguousarray(v[r])) for r in range(N)]
    return np.stack([a for a, b in q]), np.stack([mx_ref.plane(b, rng) for a, b in q])
def values_of_codes():
    e, c = np.zeros((128, 128, 4), np.float32), np.zeros((128, 2, 4), np.uint8)
    e[np.arange(128), np.arange(128), 0] = 1
    c[:127, :, 0] = np.arange(256).reshape(2, 128).T[:127]
    return mx_ref.matmul(mx_ref.quantize(e.reshape(128, 512).astype(BF)), (c.reshape(128, 8), np.full((16, 2), 127, np.uint8))).T.reshape(-1).astype(np.float64)
CODE_VALUE, SCALE_VALUE = values_of_codes(), 2.0 ** (np.arange(256) - 127.0)
def decode(q):
    return (CODE_VALUE[q[0]].reshape(16, 8, -1, 4) * SCALE_VALUE[q[1]][:, None, :, None] + 0.0).reshape(128, -1).astype(np.float32)
def f(rng, *shape):
    return mx_ref.flush((rng.standard_normal(shape, dtype=np.float32) * np.exp2(rng.integers(-2, 3, shape[:-1] + (1,)))).astype(BF))
def wide(rng, *shape, cols=0):
    v = rng.standard_normal(shape, dtype=np.float32) * np.exp2(rng.integers(-12, 13, shape)).astype(np.float32)
    if cols: v *= np.repeat(np.exp2(rng.integers(-cols, cols + 1, shape[:-2] + (1, shape[-1] // 4))) * (rng.random(shape[:-2] + (1, shape[-1] // 4)) > 0.0625), 4, axis=-1).astype(np.float32)
    return mx_ref.flush(v.astype(BF))
T, C, M = 224, 48, 2
def big(v):
    v = v.astype(np.float32)
    v[np.abs(v) < np.float32(2.0 ** -20)] = 0
    return v.astype(BF)
def numbers_of(rng):
    return {"x": big(f(rng, N, 128, 4 * T)), "u": np.array(f(rng, N, 128, 512)), "v": np.array(f(rng, N, 128, 512))}
def weights(rng, k):
    d = {}
    for n, s in (("a", k), ("c", 1.0)):
        a = mx_ref.flush((f(rng, N, 128, 256 * M).astype(np.float32) * np.float32(s)).astype(BF)).reshape(N, 8, 16, 4 * M, 16, 4)
        w = np.zeros((N, 8, 16, 4 * M, 8, 16, 4), BF)
        for g in range(8): w[:, g, :, :, g] = a[:, g]
        d[n + "c"], d[n + "p"] = packed(w.reshape(N, 128, 2048 * M), rng)
    return d
def signs(rng):
    return np.stack([rng.permutation(8) % 2 * 2.0 - 1.0 for r in range(N)])
def setup_inputs(rng):
    return {**numbers_of(rng), **weights(rng, 1.0)}
def setup_inputs_ties(rng):
    d = numbers_of(rng)
    u = d["u"].reshape(N, 128, 8, 16, 4)
    x = d["x"].reshape(N, 128, T, 4)
    for r in range(N):
        h = rng.integers(0, 8)
        for g in range(8):
            k = np.zeros(N, int) if g == h else rng.permutation(N) % 2
            a = u[r, :, g].copy()
            u[r, :, g, :N] = a[:, k]
        x[r][:, rng.permutation(T)[:T // 16]] = 0
    return {"x": x.reshape(N, 128, 4 * T), "u": u.reshape(N, 128, 512), "v": d["v"], **weights(rng, 1.0)}
def setup_inputs_near(rng):
    d = numbers_of(rng)
    x = d["x"].astype(np.float32).reshape(N, 128, T, 4)
    kind = rng.integers(0, 15, (N, T))
    x[:, 0, :, 0] = 1
    x[:, 8::8, :, 0] = kind[:, None, :] == np.arange(15)[None, :, None]
    u = d["u"].astype(np.float32).reshape(N, 128, 8, 16, 4)
    u[:, :, :, :N] = 0
    top = rng.integers(1, N, (N, 15, 8, 1))
    k = np.arange(N)
    s = np.where(k < top, 6, np.where(k == top, 7, 6 + rng.integers(0, 2, (N, 15, 8, N))))
    u[:, 0, :, :N, 0] = signs(rng)[:, :, None]
    u[:, 8::8, :, :N, 0] = s * 2.0 ** -23
    return {"x": x.reshape(N, 128, 4 * T).astype(BF), "u": u.reshape(N, 128, 512).astype(BF), "v": d["v"], **weights(rng, 1.0)}
def setup_inputs_huge(rng):
    d = numbers_of(rng)
    m = np.arange(128) // 16 % N
    kind = rng.integers(0, N, (N, T))
    below = rng.permutation(N) < N // 2
    c = np.stack([rng.permutation(T) % 2 * 2.0 - 1.0 for r in range(N)])
    c[below] = 1
    x = np.where(m[None, :, None] == kind[:, None, :], 0.875, 0.625) * c[:, None, :]
    x = 2.0 ** 30 * x[..., None] * (0.95 + 0.1 * rng.random((N, 128, T, 4)))
    p = np.stack([np.stack([rng.permutation(N) for g in range(8)]) for r in range(N)])
    a = p[:, None] == m[None, :, None, None]
    a = np.where(below[:, None, None, None], -(1 - 0.25 * a), signs(rng)[:, None, :, None] * (0.75 + 0.25 * a))
    u = d["u"].reshape(N, 128, 8, 16, 4)
    u[:, :, :, :N] = (2.0 ** 30 * a[..., None]).astype(np.float32).astype(BF)
    return {"x": x.astype(np.float32).reshape(N, 128, 4 * T).astype(BF), "u": u.reshape(N, 128, 512), "v": d["v"], **weights(rng, 2.0 ** -8)}
def setup_inputs_caps(rng):
    d = numbers_of(rng)
    o = rng.permutation(N)
    e = np.zeros((N, 8, T), int)
    for r in range(N):
        for g in range(8):
            w = rng.permutation(N)
            w = w[w != r]
            n = np.full(N, 8)
            n[w[:3]] = [C, C + 1, 0]
            n[r] = 0
            n[r] = T - np.sum(n)
            e[r, g] = rng.permutation(np.repeat(np.arange(N), n))
    e[o[0]] = o[1]
    e[o[1]] = o[1]
    x = d["x"].astype(np.float32).reshape(N, 8, 16, T, 4)
    top = e[:, :, None, :] == np.arange(N)[None, None, :, None]
    s = np.where(top, -1.0, -1.0 - 0.5 * rng.integers(1, 3, (N, 8, N, T)))
    x[:, :, :N, :, 0] = s + 3.0 * (signs(rng) > 0)[:, :, None, None]
    u = d["u"].reshape(N, 128, 8, 16, 4)
    u[:, :, :, :N] = 0
    for g in range(8):
        for k in range(N): u[:, 16 * g + k, g, k, 0] = 2.0 ** -30
    return {"x": x.reshape(N, 128, 4 * T).astype(BF), "u": u.reshape(N, 128, 512), "v": d["v"], **weights(rng, 1.0)}
def setup_inputs_spread(rng):
    d = setup_inputs(rng)
    d["x"] = big(wide(rng, N, 128, 4 * T, cols=6))
    return d
def check_inputs(d):
    b = []
    for k in ("x", "u", "v"):
        a = np.abs(d[k].astype(np.float32))
        if not (np.isfinite(a).all() and ((a == 0) | (a >= 2.0 ** -30) & (a <= 2.0 ** 30)).all()): b.append("a value of " + k)
    g = np.arange(128) // 16
    for k in ("ac", "cc"):
        a = ((d[k] & 127) != 0).reshape(-1, 128, 4 * M, 128, 4).any(axis=(0, 2, 4))
        if (a & (g[:, None] != g[None, :])).any(): b.append("a code of " + k + " outside the blocks")
        if ((d[k] & 127) == 127).any(): b.append("a code of " + k + " is no number")
    return b
def reference(x, u, v, ac, ap, cc, cp):
    took = np.full((N, N, 8, C), -1)
    slot = np.full((N, 8, T), -1)
    for r in range(N):
        s = mx_ref.matmul(mx_ref.quantize(u[r]), mx_ref.quantize(x[r])) + np.float32(0.0)
        e = np.argmax(s.reshape(8, 16, T)[:, :N], axis=1)
        for g in range(8):
            for d in range(N):
                j = np.flatnonzero(e[g] == d)[:C]
                took[r, d, g, :len(j)] = j
                slot[r, g, j] = C * d + np.arange(len(j))
    z = []
    for d in range(N):
        a, c = pk(ac[d], ap[d]), pk(cc[d], cp[d])
        q = join(*[mx_ref.quantize(gcols(x[r], took[r, d])) for r in range(N)])
        total = None
        for i in range(M):
            h = mx_ref.quantize(tile([np.maximum(mx_ref.matmul(pick(a, 512 * i + 128 * b + np.arange(128)), q), np.float32(0.0)) * np.float32(0.0625) for b in range(4)]))
            m = [mx_ref.matmul(pick(c, 512 * i + 128 * b + np.arange(128)), h) for b in range(4)]
            total = m if i == 0 else [total[b] + m[b] for b in range(4)]
        z.append(decode(mx_ref.quantize(tile([p * np.float32(0.0625) for p in total]))).astype(BF))
    y, ol = np.zeros((N, 128, T), np.float32), np.zeros((N, 8, T), np.float32)
    oc, osc = np.zeros((N, 128, 4 * T), np.uint8), np.zeros((N, 16, T), np.uint8)
    for r in range(N):
        came = np.concatenate([cut(z[d], r, 4 * C) for d in range(N)], axis=1)
        q = mx_ref.quantize((x[r].astype(np.float32) + gcols(came, slot[r]).astype(np.float32)).astype(BF))
        y[r] = mx_ref.matmul(mx_ref.quantize(v[r]), q)
        ol[r] = slot[r]
        oc[r], osc[r] = emit(q)
    return {"y": y, "ol": ol, "oc": oc, "osc": osc}

@@ -1,0 +1,407 @@
+from concourse.bass import DstId, RemoteDMATransfer
+from concourse.mybir import dt, AluOpType, ActivationFunctionType
+
+N, TC, C = 8, 224, 48
+HALF = 4 * C
+BIG = 4096.0
+STRIDE = 512
+HW = 8 * C + TC
+F8, U8, U16, BF, F32, I32 = "float8_e4m3fn_x4", "uint8", "uint16", "bfloat16", "float32", "int32"
+
+
+def _sb(n, d):
+    return ("sbuf", [128, n], d)
+
+
+SCRATCH = {
+    "ps": ("psum", [128, 4096], F32),
+    "xs": _sb(4 * TC, BF), "us": _sb(512, BF), "vs": _sb(512, BF),
+    "xq": _sb(TC, F8), "xp": _sb(TC, U8), "uq": _sb(128, F8), "up": _sb(128, U8),
+    "uq2": _sb(128, F8), "up2": _sb(128, U8), "vq": _sb(128, F8), "vp": _sb(128, U8),
+    "aq": _sb(1024, F8), "apl": _sb(1024, U8), "cq": _sb(1024, F8), "cpl": _sb(1024, U8),
+    "pidx": _sb(8, I32), "i16": _sb(8, I32), "t0": _sb(8, I32), "t1": _sb(8, I32), "uoff": _sb(8, U16),
+    "pc": _sb(128, F32), "pcT": _sb(128, F32), "i32c": _sb(8, F32), "off9": _sb(8, U16), "selo": _sb(2, U16),
+    "jv": _sb(TC, BF), "pmax": _sb(TC, F32), "ptwo": _sb(TC, BF),
+    "pt": _sb(TC, F32), "rm": _sb(TC, F32), "hit": _sb(TC, BF), "st": _sb(TC, BF), "stT": _sb(TC, BF),
+    "av": _sb(TC, F32), "bv": _sb(TC + 8, BF), "val": _sb(TC + 32, F32), "ff": _sb(2 * TC + 32, F32),
+    "g9": _sb(112, F32), "r9": _sb(112, F32), "sl": _sb(16, U16),
+    "win": _sb(4 * STRIDE, BF), "w2": _sb(4 * 224, BF), "il": _sb(32, U16),
+    "xpl": _sb(4 * TC, BF), "xt": _sb(8 * HALF, BF),
+    "x1q": _sb(HALF, F8), "x1p": _sb(HALF, U8), "x1lq": _sb(HALF, F8), "x1lp": _sb(HALF, U8),
+    "x2q": _sb(10 * C, F8), "x2p": _sb(10 * C, U8),
+    "z1q": _sb(HALF, F8), "z1p": _sb(HALF, U8), "z1lq": _sb(HALF, F8), "z1lp": _sb(HALF, U8),
+    "z2q": _sb(10 * C, F8), "z2p": _sb(10 * C, U8),
+    "rxq": _sb(2 * C, F8), "rxp": _sb(2 * C, U8), "rzq": _sb(2 * C, F8), "rzp": _sb(2 * C, U8),
+    "ht": _sb(16 * HALF, BF), "hq": _sb(4 * HALF, F8), "hp": _sb(4 * HALF, U8), "zt": _sb(8 * HALF, BF),
+    "et": _sb(2048, BF), "eq": _sb(512, F8), "ep": _sb(512, U8), "pcol": _sb(2, F32),
+    "hw": _sb(4 * HW, BF), "tab": _sb(HW, F32), "olb": _sb(TC, F32),
+    "d0": _sb(16, I32), "d1": _sb(16, I32), "d2": _sb(16, I32), "d3": _sb(16, F32), "d4": _sb(16, F32),
+    "d5": _sb(16, F32), "d6": _sb(16, F32), "d7": _sb(16, F32), "d8": _sb(16, F32), "d9": _sb(16, F32),
+    "da": _sb(16, F32), "db": _sb(16, F32), "dc": _sb(16, I32), "dd": _sb(2, I32), "de": _sb(2, F32), "hl": _sb(16, U16),
+    "yt": _sb(4 * TC, BF), "yq": _sb(TC, F8), "yp": _sb(TC, U8), "yo": _sb(TC, F32),
+}
+SEMAPHORES = ["sent", "xfar", "xnear", "zfar", "znear", "rx", "rz"] + ["e%d" % k for k in range(140)]
+
+
+def _mask(engines):
+    m = 0
+    for e in engines:
+        m |= 1 << e
+    return m
+
+
+def _plan(T, topo):
+    cores = T.cores
+    plan = []
+    for r in range(N):
+        far = [d for d in range(N) if d != r and not topo.may_write(cores[r], cores[d])]
+        near = [d for d in range(N) if d not in far]
+        assert len(far) == 4 and all(s[k + 2] == s[k] + N // 2 for s in (far, near) for k in range(2))
+        fp = [[far[0], far[2]], [far[1], far[3]]]
+        if near.index(r) % 2:
+            fp = fp[::-1]
+        npair = [[near[0], near[2]], [near[1], near[3]]]
+        mine = [p for p in npair if r in p][0]
+        other = [p for p in npair if r not in p][0]
+        first = mine[0] == r
+        order = fp[0] + fp[1] + (mine + other if first else other + mine)
+        able = [c for c in topo.cores_of(cores[r]) if c not in cores and all(topo.may_write(c, cores[d]) for d in far)]
+        same = [c for c in able if topo.die(c) == topo.die(cores[r])]
+        across = [c for c in able if topo.die(c) != topo.die(cores[r])]
+        plan.append({"order": order, "first": first, "codes": [same[0], across[0]], "scales": [same[1], across[1]],
+                     "near": [d for d in order[4:] if d != r]})
+    return plan
+
+
+def _near_masks(topo, src, dst):
+    e = topo.engines(src, dst)
+    h, q = len(e) // 2, len(e) // 4
+    return [e[:h], e[h:h + q], e[h + q:]], [e[:q], e[q:h], e[h:]]
+
+
+def _dst(topo, dst, src):
+    rid, pid = topo.addr(dst, src)
+    return DstId(rid=rid, pnc=pid)
+
+
+def _u8(v):
+    return v.bitcast(dt.uint8)
+
+
+def _helper(g, core, T, topo, plan):
+    for r in range(N):
+        for kind in ("codes", "scales"):
+            if core in plan[r][kind]:
+                t = plan[r][kind].index(core)
+                came = len(topo.engines(T.cores[r], core)) // 2
+                total = 0
+                for stage in ("x", "z"):
+                    g.wait_ge(T.sem["r" + stage], came)
+                    tr = []
+                    for k in range(2):
+                        d = plan[r]["order"][2 * t + k]
+                        e = topo.engines(core, T.cores[d])
+                        e = e[k * (len(e) // 2):(k + 1) * (len(e) // 2)]
+                        at = C * plan[d]["order"].index(r)
+                        if kind == "codes":
+                            src, dst = _u8(T["r%sq" % stage][:, C * k:C * k + C]), _u8(T[stage + "1lq"][:, at:at + C])
+                        else:
+                            src, dst = T["r%sp" % stage][:, C * k:C * k + C], T[stage + "1lp"][:, at:at + C]
+                        tr.append(RemoteDMATransfer(dst_ids=[_dst(topo, T.cores[d], core)], dma_engine_mask=_mask(e),
+                                                    remote_sem=T.sem[stage + "far"], src=src, dst=dst))
+                        total += len(e)
+                    g.remote_dma_fused(tr, local_sem=T.sem.sent)
+                g.wait_ge(T.sem.sent, total)
+
+
+def rank_program(g, core, T, topo):
+    plan = _plan(T, topo)
+    r = T.rank_of(core)
+    if r is None:
+        _helper(g, core, T, topo, plan)
+        return
+    me = plan[r]
+    order = me["order"]
+    V, S, PE, Q = g.vector, g.scalar, g.tensor, g.sync
+    queues = {"g": g, "v": V, "s": S, "t": PE, "q": Q}
+    A, ACT = AluOpType, ActivationFunctionType
+    top, seen, used = {}, {}, [0]
+
+    def wait(q, e):
+        if seen.get((q, e[0]), 0) < e[1]:
+            queues[q].wait_ge(T.sem[e[0]], e[1])
+            seen[(q, e[0])] = e[1]
+
+    def op(q, call, deps=(), join=None, on=None, inc=1):
+        for e in deps:
+            wait(q, e)
+        if on is not None:
+            wait(q, on)
+            assert top[on[0]] == on[1]
+            e = [on[0], on[1]]
+        elif join is not None:
+            e = join
+        else:
+            e = ["e%d" % used[0], 0]
+            used[0] += 1
+        call().then_inc(T.sem[e[0]], inc)
+        e[1] += inc
+        top[e[0]] = e[1]
+        return e
+
+    def bank(k, n):
+        return T.ps[:, 512 * k:512 * k + n]
+
+    def iota(out, pattern, base, cm=0, join=None, deps=()):
+        if out.dtype == T.pidx.dtype:
+            return op("g", lambda: g.iota(out, pattern, base, cm), deps, join=join)
+        return op("g", lambda: g.iota(out, pattern, base, cm, allow_small_or_imprecise_dtypes=True), deps, join=join)
+
+    l_u = op("s", lambda: S.dma_start(T.us[:], T.u[:]), inc=16)
+    l_x = op("q", lambda: Q.dma_start(T.xs[:], T.x[:]), inc=16)
+    l_a = op("q", lambda: Q.dma_start(_u8(T.aq[:]), T.ac[:]), inc=16)
+    op("q", lambda: Q.dma_start(T.apl[:], T.ap[:]), join=l_a, inc=16)
+    l_c = op("q", lambda: Q.dma_start(_u8(T.cq[:]), T.cc[:]), inc=16)
+    op("q", lambda: Q.dma_start(T.cpl[:], T.cp[:]), join=l_c, inc=16)
+    l_v = op("q", lambda: Q.dma_start(T.vs[:], T.v[:]), inc=16)
+
+    c_p = iota(T.pidx[:], [[0, 8]], 0, 1)
+    iota(T.i16[:], [[16, 8]], 0, join=c_p)
+    c_pc = iota(T.pc[:, 0:32], [[0, 4], [2, 2], [0, 4]], int(BIG) - 1)
+    for d in range(N // 2):
+        iota(T.pc[:, 32 + d:64:4], [[0, 4], [-1, 2]], STRIDE * (order.index(d) // 2) + STRIDE // 2, join=c_pc)
+    for k, add in enumerate((8, TC + 32, TC + 8, 0)):
+        iota(T.pc[:, 64 + 8 * k:72 + 8 * k], [[1, 8]], 8 * k + add, join=c_pc)
+    for h in range(2):
+        for par in range(2):
+            base = 16 * h + (0 if par == h else 96 + 32 * (1 - h))
+            iota(T.pc[:, 96 + 16 * h + par:96 + 16 * h + 12:2], [[224, 2], [32, 3]], base, join=c_pc)
+    iota(T.i32c[:], [[32, 8]], 0, join=c_pc)
+    c_j = iota(T.jv[:], [[1, TC]], 0)
+
+    m0 = op("v", lambda: V.memset(T.pmax[:], 0.0))
+    op("v", lambda: V.memset(T.ptwo[:], 2.0), join=m0)
+    m1 = op("v", lambda: V.memset(T.pc[:, 108:112], 0.0))
+    op("v", lambda: V.memset(T.pc[:, 124:128], 0.0), join=m1)
+    op("v", lambda: V.memset(T.val[:, 0:16], 0.0), join=m1)
+    op("v", lambda: V.memset(T.val[:, 16 + TC:32 + TC], 0.0), join=m1)
+    op("v", lambda: V.memset(T.bv[:, 0:1], 0.0), join=m1)
+    for t in range(4):
+        op("v", lambda: V.memset(T.win[:, STRIDE * t + 192:STRIDE * t + 320], 0.0), join=m1)
+    op("v", lambda: V.memset(T.pmax[:, 0:TC:16], -1e29), [m0], join=m1)
+    op("v", lambda: V.memset(T.ptwo[:, 8:TC:16], 0.0), join=m1)
+    e = op("v", lambda: V.tensor_scalar(T.t0[:], T.pidx[:], 7, None, A.bitwise_and), [c_p])
+    e = op("v", lambda: V.tensor_tensor(T.t1[:], T.t0[:], T.i16[:], A.add), on=e)
+    c_uo = op("v", lambda: V.tensor_copy(T.uoff[:], T.t1[:]), on=e)
+
+    q_u = op("v", lambda: V.quantize_mx(T.uq[:], T.up[:], T.us[:]), [l_u])
+    k_u = op("v", lambda: V.tensor_copy(T.uq2[:, 0:128].bitcast(dt.uint32), T.uq[:, 0:128].bitcast(dt.uint32).indirect(T.uoff[:, 0:8])), [q_u, c_uo])
+    k_s = op("s", lambda: S.activation(T.up2[:, 0:128], T.up[:, 0:128].indirect(T.uoff[:, 0:8]), ACT.Copy), [q_u, c_uo])
+    q_x = op("v", lambda: V.quantize_mx(T.xq[:], T.xp[:], T.xs[:]), [l_x])
+    m_p = op("t", lambda: PE.matmul_mx(bank(0, TC), T.uq2[:], T.up2[:], T.xq[:], T.xp[:], True, True), [k_u, k_s, q_x])
+    pl = None
+    for t in range(4):
+        pl = op("s", lambda: S.activation(T.xpl[:, TC * t:TC * t + TC], T.xs[:, t:4 * TC:4], ACT.Copy), [l_x], join=pl)
+    c_t = op("v", lambda: V.transpose(T.pcT[:], T.pc[:]), [c_pc, m1])
+    c_o = op("v", lambda: V.tensor_scalar(T.off9[:], T.i32c[:], T.pcT[:, 64:65], None, A.add), [c_t])
+    op("v", lambda: V.tensor_copy(T.selo[:], T.pcT[:, 96:98]), join=c_o)
+
+    e = op("v", lambda: V.transpose(T.pt[:], bank(0, TC)), [m_p])
+    e = op("v", lambda: V.tensor_tensor_scan(T.rm[:], T.pmax[:], T.pt[:], 0.0, A.add, A.max), on=e)
+    e = op("v", lambda: V.tensor_tensor(T.hit[:], T.pt[:], T.rm[:], A.is_equal), on=e)
+    e = op("v", lambda: V.tensor_tensor_scan(T.st[:], T.ptwo[:], T.hit[:], 0.0, A.mult, A.add), on=e)
+    e = op("v", lambda: V.transpose(T.stT[:], T.st[:]), on=e)
+    e = op("v", lambda: V.tensor_scalar(T.av[:], T.stT[:], 1.0, T.pcT[:, 0:1], A.is_equal, A.mult), [e])
+    op("v", lambda: V.tensor_scalar(T.bv[:, 1:TC + 1], T.stT[:], 1.0, BIG, A.is_equal, A.mult), join=e)
+    e = op("v", lambda: V.tensor_tensor_scan(T.val[:, 16:16 + TC], T.av[:], T.bv[:, 0:TC], T.pcT[:, 32:33], A.add, A.subtract), on=e)
+    e = op("v", lambda: V.transpose(T.ff[:, 0:TC], T.val[:, 16:16 + TC]), [e])
+    op("v", lambda: V.transpose(T.ff[:, TC:2 * TC + 32], T.val[:]), join=e)
+    e = op("v", lambda: V.tensor_copy(T.g9[:], T.ff[:, 0:2 * TC + 32].indirect(T.off9[:, 0:7])), [c_o], on=e)
+    e_r9 = op("v", lambda: V.tensor_tensor_scan(T.r9[:], T.pmax[:, 0:TC:2], T.g9[:], 0.0, A.add, A.max), on=e)
+    e = op("v", lambda: V.tensor_scalar(T.sl[:, 0:14], T.r9[:, 7:112:8], -BIG, None, A.add), on=e_r9)
+    e_sc = op("v", lambda: V.tensor_copy(T.win[:, 0:4 * STRIDE].indirect(T.sl[:, 0:14]), T.jv[:]), [c_j], on=e)
+
+    sent = [0]
+
+    def send_far(stage, dep):
+        wait("g", dep)
+        for kind in ("codes", "scales"):
+            tr = []
+            for t in range(2):
+                c = me[kind][t]
+                eng = topo.engines(core, c)[t::2]
+                if kind == "codes":
+                    src, dst = _u8(T[stage + "1q"][:, 2 * C * t:2 * C * (t + 1)]), _u8(T["r%sq" % stage][:])
+                else:
+                    src, dst = T[stage + "1p"][:, 2 * C * t:2 * C * (t + 1)], T["r%sp" % stage][:]
+                tr.append(RemoteDMATransfer(dst_ids=[_dst(topo, c, core)], dma_engine_mask=_mask(eng), remote_sem=T.sem["r" + stage], src=src, dst=dst))
+                sent[0] += len(eng)
+            g.remote_dma_fused(tr, local_sem=T.sem.sent)
+
+    def own_first(k, stage):
+        return plan[k]["first"] == (stage == "x")
+
+    def send_near(stage, dep):
+        wait("g", dep)
+        for kind in range(2):
+            tr = []
+            for k, d in enumerate(me["near"]):
+                eng = _near_masks(topo, core, T.cores[d])[kind][k]
+                a = 3 * C + C * (k + (1 if own_first(r, stage) else 0))
+                b = (0 if own_first(d, stage) else 7 * C) + C * plan[d]["near"].index(r)
+                if kind == 0:
+                    src, dst = _u8(T[stage + "2q"][:, a:a + C]), _u8(T[stage + "2q"][:, b:b + C])
+                else:
+                    src, dst = T[stage + "2p"][:, a:a + C], T[stage + "2p"][:, b:b + C]
+                tr.append(RemoteDMATransfer(dst_ids=[_dst(topo, T.cores[d], core)], dma_engine_mask=_mask(eng), remote_sem=T.sem[stage + "near"], src=src, dst=dst))
+                sent[0] += len(eng)
+            g.remote_dma_fused(tr, local_sem=T.sem.sent)
+
+    far_count = sum(2 * (len(topo.engines(plan[s]["codes"][0], core)) // 2) for s in order[:4])
+    near_count = 0
+    for s in me["near"]:
+        mk = _near_masks(topo, T.cores[s], core)
+        near_count += len(mk[0][plan[s]["near"].index(r)]) + len(mk[1][plan[s]["near"].index(r)])
+
+    def near_view(stage):
+        a = 0 if own_first(r, stage) else 6 * C
+        return T[stage + "2q"][:, a:a + HALF], T[stage + "2p"][:, a:a + HALF]
+
+    q_b = []
+    for hf in range(2):
+        e = None
+        for t in (2 * hf, 2 * hf + 1):
+            c0 = STRIDE * t + STRIDE // 2
+            e = op("v", lambda: V.transpose(T.w2[:, 224 * t:224 * t + 96], T.win[:, c0 - 48:c0 + 48]), [e_sc], join=e)
+            op("v", lambda: V.transpose(T.w2[:, 224 * t + 96:224 * t + 224], T.win[:, c0 - 64:c0 + 64]), join=e)
+        e_il = op("v", lambda: V.tensor_scalar(T.il[:, 16 * hf:16 * hf + 16], T.w2[:, 448 * hf:448 * hf + 448].indirect(T.selo[:, 0:1]), 0.0, None, A.add), on=e)
+        lst = T.il[:, 16 * hf:16 * hf + 12]
+        lo = 4 * HALF * hf
+        gv = gs = None
+        for t in range(2):
+            gs = op("s", lambda: S.activation(T.xt[:, lo + 2 + t:lo + 4 * HALF:4], T.xpl[:, TC * (2 + t):TC * (3 + t)].indirect(lst), ACT.Copy), [e_il, pl], join=gs)
+            gv = op("v", lambda: V.tensor_copy(T.xt[:, lo + t:lo + 4 * HALF:4], T.xpl[:, TC * t:TC * (t + 1)].indirect(lst)), [e_il, pl], join=gv)
+        oq, osc = (T.x1q[:], T.x1p[:]) if hf == 0 else (T.x2q[:, 3 * C:7 * C], T.x2p[:, 3 * C:7 * C])
+        q_b.append(op("v", lambda: V.quantize_mx(oq, osc, T.xt[:, lo:lo + 4 * HALF]), [gs], on=gv))
+        (send_far if hf == 0 else send_near)("x", q_b[hf])
+
+    c_tab = None
+    for pos in range(N):
+        if pos % 2 == 0:
+            c_tab = iota(T.tab[:, C * pos:C * pos + C], [[-1, C]], C * order[pos] + C - 1, join=c_tab)
+        else:
+            c_tab = iota(T.tab[:, C * pos:C * pos + C], [[1, C]], C * order[pos], join=c_tab)
+    iota(T.tab[:, N * C:HW], [[0, TC]], -1, join=c_tab)
+    c_d = iota(T.pcol[:], [[0, 2]], 0, 1)
+    iota(T.dc[:], [[16, 16]], N * C, join=c_d)
+
+    q_v = op("v", lambda: V.quantize_mx(T.vq[:], T.vp[:], T.vs[:]), [l_v])
+    e_z = op("v", lambda: V.memset(T.et[:], 0.0))
+    h_x = None
+    for t in range(4):
+        h_x = op("v", lambda: V.tensor_copy(T.hw[:, HW * t + N * C:HW * (t + 1)], T.xpl[:, TC * t:TC * (t + 1)]), join=h_x)
+    n14 = slice(0, 14)
+    e = op("v", lambda: V.tensor_scalar(T.d0[:, n14], T.r9[:, 7:112:8], -BIG, None, A.add), [e_r9])
+    op("v", lambda: V.tensor_scalar(T.dd[:], T.pidx[:, 0:2], 15, None, A.bitwise_and), join=e)
+    e = op("v", lambda: V.tensor_scalar(T.d1[:, n14], T.d0[:, n14], 9, None, A.logical_shift_right), [e])
+    op("v", lambda: V.tensor_scalar(T.d2[:, n14], T.d0[:, n14], STRIDE - 1, None, A.bitwise_and), join=e)
+    op("v", lambda: V.tensor_copy(T.de[:], T.dd[:]), join=e)
+    e = op("v", lambda: V.tensor_scalar(T.d3[:, n14], T.d1[:, n14], 2.0 * C, float(C - STRIDE // 2), A.mult, A.add), [e])
+    op("v", lambda: V.tensor_scalar(T.d4[:, n14], T.d2[:, n14], 0.5 - STRIDE // 2, None, A.add), join=e)
+    op("v", lambda: V.tensor_scalar(T.d5[:, n14], T.dc[:, n14], T.de[:, 0:1], None, A.add), [c_d], join=e)
+    e = op("v", lambda: V.tensor_tensor(T.d6[:, n14], T.d3[:, n14], T.d2[:, n14], A.add), [e])
+    op("v", lambda: V.tensor_tensor(T.d7[:, n14], T.d4[:, n14], T.d4[:, n14], A.mult), join=e)
+    e = op("v", lambda: V.tensor_tensor(T.d8[:, n14], T.d6[:, n14], T.d5[:, n14], A.subtract), [e])
+    op("v", lambda: V.tensor_scalar(T.d9[:, n14], T.d7[:, n14], float(C * C), None, A.is_lt), join=e)
+    e = op("v", lambda: V.tensor_tensor(T.da[:, n14], T.d8[:, n14], T.d9[:, n14], A.mult), on=e)
+    e = op("v", lambda: V.tensor_tensor(T.db[:, n14], T.da[:, n14], T.d5[:, n14], A.add), on=e)
+    e_hl = op("v", lambda: V.tensor_copy(T.hl[:, n14], T.db[:, n14]), on=e)
+    e = None
+    for b in range(4):
+        e = op("v", lambda: V.tensor_scalar(T.et[:, 512 * b + b:512 * (b + 1):4], T.jv[:, 0:128], T.pcol[:, 0:1], None, A.is_equal), [e_z, c_d], join=e)
+    q_e = op("v", lambda: V.quantize_mx(T.eq[:], T.ep[:], T.et[:]), on=e)
+    e = op("s", lambda: S.activation(T.olb[:], T.tab[:, 0:HW].indirect(T.hl[:, n14]), ACT.Copy), [e_hl, c_tab])
+    stores = op("q", lambda: Q.dma_start(T.ol[:], T.olb[0:128:16, :]), [e], inc=16)
+
+    def evacuate(q, out, src, relu, dep, join):
+        if q == "s":
+            return op("s", lambda: S.activation(out, src, ACT.Relu if relu else ACT.Identity, scale=0.0625), [dep], join=join)
+        if relu:
+            return op("v", lambda: V.tensor_scalar(out, src, 0.0, 0.0625, A.max, A.mult), [dep], join=join)
+        return op("v", lambda: V.tensor_scalar(out, src, 0.0625, None, A.mult), [dep], join=join)
+
+    q_z = []
+    for hf in range(2):
+        xc, xp = (T.x1lq[:], T.x1lp[:]) if hf == 0 else near_view("x")
+        wait("t", l_a)
+        if hf == 0:
+            wait("t", e_r9)
+            PE.wait_ge(T.sem.xfar, far_count)
+        else:
+            wait("t", q_b[1])
+            PE.wait_ge(T.sem.xnear, near_count)
+        q_h = []
+        for i in range(2):
+            b0 = 4 * ((i + hf) % 2)
+            if hf == 1 and i == 1:
+                wait("t", q_z[0])
+            k = 2 * hf + i
+            done = {"s": None, "v": None}
+            for b in range(4):
+                w = 512 * i + 128 * b
+                m = op("t", lambda: PE.matmul_mx(bank(b0 + b, HALF), T.aq[:, w:w + 128], T.apl[:, w:w + 128], xc, xp, True, True))
+                q = ("svsv", "sssv")[i][b]
+                done[q] = evacuate(q, T.ht[:, 4 * HALF * k + b:4 * HALF * (k + 1):4], bank(b0 + b, HALF), True, m, done[q])
+            q_h.append(op("v", lambda: V.quantize_mx(T.hq[:, HALF * k:HALF * (k + 1)], T.hp[:, HALF * k:HALF * (k + 1)],
+                                                     T.ht[:, 4 * HALF * k:4 * HALF * (k + 1)]), [done["s"]], on=done["v"]))
+        b0 = 4 * hf
+        wait("t", l_c)
+        done = {"s": None, "v": None}
+        for i in range(2):
+            k = 2 * hf + i
+            wait("t", q_h[i])
+            for b in range(4):
+                w = 512 * i + 128 * b
+                call = lambda: PE.matmul_mx(bank(b0 + b, HALF), T.cq[:, w:w + 128], T.cpl[:, w:w + 128],
+                                            T.hq[:, HALF * k:HALF * (k + 1)], T.hp[:, HALF * k:HALF * (k + 1)], i == 0, i == 1)
+                if i == 0:
+                    call()
+                else:
+                    m = op("t", call)
+                    q = "svsv"[b]
+                    done[q] = evacuate(q, T.zt[:, 4 * HALF * hf + b:4 * HALF * (hf + 1):4], bank(b0 + b, HALF), False, m, done[q])
+        oq, osc = (T.z1q[:], T.z1p[:]) if hf == 0 else (T.z2q[:, 3 * C:7 * C], T.z2p[:, 3 * C:7 * C])
+        q_z.append(op("v", lambda: V.quantize_mx(oq, osc, T.zt[:, 4 * HALF * hf:4 * HALF * (hf + 1)]), [done["s"]], on=done["v"]))
+        (send_far if hf == 0 else send_near)("z", q_z[hf])
+
+    added = {}
+    wait("t", q_e)
+    for hf in range(2):
+        zc, zp = (T.z1lq[:], T.z1lp[:]) if hf == 0 else near_view("z")
+        if hf == 0:
+            PE.wait_ge(T.sem.zfar, far_count)
+        else:
+            wait("t", q_z[1])
+            PE.wait_ge(T.sem.znear, near_count)
+        for b in range(4):
+            m = op("t", lambda: PE.matmul_mx(bank(4 * hf + b, HALF), T.eq[:, 128 * b:128 * b + 128], T.ep[:, 128 * b:128 * b + 128], zc, zp, True, True))
+            lo = 4 * HALF * hf
+            added[(hf, b)] = op("v", lambda: V.tensor_tensor(T.hw[:, HW * b + HALF * hf:HW * b + HALF * (hf + 1)], bank(4 * hf + b, HALF),
+                                                             T.xt[:, lo + b:lo + 4 * HALF:4], A.add), [m], join=added.get((0, 0)) if hf == 0 else None)
+    gs = None
+    for b in range(3):
+        gs = op("s", lambda: S.activation(T.yt[:, b:4 * TC:4], T.hw[:, HW * b:HW * (b + 1)].indirect(T.hl[:, n14]), ACT.Copy),
+                [h_x, added[(0, 0)], added[(1, b)]], join=gs)
+    gv = op("v", lambda: V.tensor_copy(T.yt[:, 3:4 * TC:4], T.hw[:, HW * 3:HW * 4].indirect(T.hl[:, n14])), [h_x, added[(0, 0)], e_hl], on=added[(1, 3)])
+    q_y = op("v", lambda: V.quantize_mx(T.yq[:], T.yp[:], T.yt[:]), [gs], on=gv)
+    m = op("t", lambda: PE.matmul_mx(bank(0, TC), T.vq[:], T.vp[:], T.yq[:], T.yp[:], True, True), [q_v, q_y])
+    op("q", lambda: Q.dma_start(T.oc[:], _u8(T.yq[:])), [q_y], join=stores, inc=16)
+    for k in range(4):
+        q = "qqss"[k]
+        op(q, lambda: queues[q].dma_start(T.osc[4 * k:4 * k + 4, :], T.yp[32 * k:32 * k + 4, :]), [q_y], join=stores, inc=16)
+    e = op("v", lambda: V.tensor_copy(T.yo[:], bank(0, TC)), [m])
+    op("s", lambda: S.dma_start(T.y[:], T.yo[:]), [e], join=stores, inc=16)
+    g.wait_ge(T.sem.sent, sent[0])
+    for name in top:
+        if max([seen.get((q, name), 0) for q in queues]) < top[name]:
+            wait("g", [name, top[name]])

@@ -28,19 +28,20 @@ SCRATCH = {
     "win": _sb(4 * STRIDE, BF), "w2": _sb(4 * 224, BF), "il": _sb(32, U16),
     "xpl": _sb(4 * TC, BF), "xt": _sb(8 * HALF, BF),
     "x1q": _sb(HALF, F8), "x1p": _sb(HALF, U8), "x1lq": _sb(HALF, F8), "x1lp": _sb(HALF, U8),
-    "x2q": _sb(10 * C, F8), "x2p": _sb(10 * C, U8),
+    "x2q": _sb(HALF, F8), "x2p": _sb(HALF, U8), "x2lq": _sb(3 * C, F8), "x2lp": _sb(3 * C, U8),
+    "z0q": _sb(128, F8), "z0p": _sb(128, U8),
     "z1q": _sb(HALF, F8), "z1p": _sb(HALF, U8), "z1lq": _sb(HALF, F8), "z1lp": _sb(HALF, U8),
-    "z2q": _sb(10 * C, F8), "z2p": _sb(10 * C, U8),
+    "z2q": _sb(3 * C, F8), "z2p": _sb(3 * C, U8), "z2lq": _sb(3 * C, F8), "z2lp": _sb(3 * C, U8),
     "rxq": _sb(2 * C, F8), "rxp": _sb(2 * C, U8), "rzq": _sb(2 * C, F8), "rzp": _sb(2 * C, U8),
-    "ht": _sb(16 * HALF, BF), "hq": _sb(4 * HALF, F8), "hp": _sb(4 * HALF, U8), "zt": _sb(8 * HALF, BF),
-    "et": _sb(2048, BF), "eq": _sb(512, F8), "ep": _sb(512, U8), "pcol": _sb(2, F32),
+    "ht": _sb(24 * HALF, BF), "hq": _sb(6 * HALF, F8), "hp": _sb(6 * HALF, U8), "zt": _sb(12 * HALF, BF),
+    "eb": _sb(516, BF), "et": _sb(2048, BF), "eq": _sb(512, F8), "ep": _sb(512, U8),
     "hw": _sb(4 * HW, BF), "tab": _sb(HW, F32), "olb": _sb(TC, F32),
     "d0": _sb(16, I32), "d1": _sb(16, I32), "d2": _sb(16, I32), "d3": _sb(16, F32), "d4": _sb(16, F32),
     "d5": _sb(16, F32), "d6": _sb(16, F32), "d7": _sb(16, F32), "d8": _sb(16, F32), "d9": _sb(16, F32),
     "da": _sb(16, F32), "db": _sb(16, F32), "dc": _sb(16, I32), "dd": _sb(2, I32), "de": _sb(2, F32), "hl": _sb(16, U16),
     "yt": _sb(4 * TC, BF), "yq": _sb(TC, F8), "yp": _sb(TC, U8), "yo": _sb(TC, F32),
 }
-SEMAPHORES = ["sent", "xfar", "xnear", "zfar", "znear", "rx", "rz"] + ["e%d" % k for k in range(140)]
+SEMAPHORES = ["sent", "xfar", "xnear", "zfar", "znear", "rx", "rz"] + ["e%d" % k for k in range(143)]
 
 
 def _mask(engines):
@@ -149,15 +150,15 @@ def rank_program(g, core, T, topo):
         top[e[0]] = e[1]
         return e
 
-    def bank(k, n):
-        return T.ps[:, 512 * k:512 * k + n]
+    def bank(k, n, at=0):
+        return T.ps[:, 512 * k + at:512 * k + at + n]
 
     def iota(out, pattern, base, cm=0, join=None, deps=()):
         if out.dtype == T.pidx.dtype:
             return op("g", lambda: g.iota(out, pattern, base, cm), deps, join=join)
         return op("g", lambda: g.iota(out, pattern, base, cm, allow_small_or_imprecise_dtypes=True), deps, join=join)
 
-    l_u = op("s", lambda: S.dma_start(T.us[:], T.u[:]), inc=16)
+    l_u = op("q", lambda: Q.dma_start(T.us[:], T.u[:]), inc=16)
     l_x = op("q", lambda: Q.dma_start(T.xs[:], T.x[:]), inc=16)
     l_a = op("q", lambda: Q.dma_start(_u8(T.aq[:]), T.ac[:]), inc=16)
     op("q", lambda: Q.dma_start(T.apl[:], T.ap[:]), join=l_a, inc=16)
@@ -165,6 +166,7 @@ def rank_program(g, core, T, topo):
     op("q", lambda: Q.dma_start(T.cpl[:], T.cp[:]), join=l_c, inc=16)
     l_v = op("q", lambda: Q.dma_start(T.vs[:], T.v[:]), inc=16)
 
+    m_e = op("v", lambda: V.memset(T.eb[:], 1.0))
     c_p = iota(T.pidx[:], [[0, 8]], 0, 1)
     iota(T.i16[:], [[16, 8]], 0, join=c_p)
     c_pc = iota(T.pc[:, 0:32], [[0, 4], [2, 2], [0, 4]], int(BIG) - 1)
@@ -177,7 +179,9 @@ def rank_program(g, core, T, topo):
             base = 16 * h + (0 if par == h else 96 + 32 * (1 - h))
             iota(T.pc[:, 96 + 16 * h + par:96 + 16 * h + 12:2], [[224, 2], [32, 3]], base, join=c_pc)
     iota(T.i32c[:], [[32, 8]], 0, join=c_pc)
+    c_e = op("g", lambda: g.affine_select(T.eb[:], T.eb[:], [[1, 516]], A.is_equal, 0.0, -3, -4), [m_e])
     c_j = iota(T.jv[:], [[1, TC]], 0)
+    c_d = iota(T.dc[:], [[16, 16]], N * C)
 
     m0 = op("v", lambda: V.memset(T.pmax[:], 0.0))
     op("v", lambda: V.memset(T.ptwo[:], 2.0), join=m0)
@@ -202,26 +206,31 @@ def rank_program(g, core, T, topo):
     pl = None
     for t in range(4):
         pl = op("s", lambda: S.activation(T.xpl[:, TC * t:TC * t + TC], T.xs[:, t:4 * TC:4], ACT.Copy), [l_x], join=pl)
-    c_t = op("v", lambda: V.transpose(T.pcT[:], T.pc[:]), [c_pc, m1])
-    c_o = op("v", lambda: V.tensor_scalar(T.off9[:], T.i32c[:], T.pcT[:, 64:65], None, A.add), [c_t])
-    op("v", lambda: V.tensor_copy(T.selo[:], T.pcT[:, 96:98]), join=c_o)
+    e_t = None
+    for b in range(4):
+        e_t = op("s", lambda: S.activation(T.et[:, 512 * b:512 * (b + 1)], T.eb[:, 3 - b:515 - b], ACT.Copy), [c_e], join=e_t)
 
-    e = op("v", lambda: V.transpose(T.pt[:], bank(0, TC)), [m_p])
+    e = op("v", lambda: V.transpose(T.pt[:], bank(0, TC)), [m_p, m1])
     e = op("v", lambda: V.tensor_tensor_scan(T.rm[:], T.pmax[:], T.pt[:], 0.0, A.add, A.max), on=e)
     e = op("v", lambda: V.tensor_tensor(T.hit[:], T.pt[:], T.rm[:], A.is_equal), on=e)
     e = op("v", lambda: V.tensor_tensor_scan(T.st[:], T.ptwo[:], T.hit[:], 0.0, A.mult, A.add), on=e)
     e = op("v", lambda: V.transpose(T.stT[:], T.st[:]), on=e)
+    op("v", lambda: V.transpose(T.pcT[:], T.pc[:]), [c_pc], join=e)
     e = op("v", lambda: V.tensor_scalar(T.av[:], T.stT[:], 1.0, T.pcT[:, 0:1], A.is_equal, A.mult), [e])
     op("v", lambda: V.tensor_scalar(T.bv[:, 1:TC + 1], T.stT[:], 1.0, BIG, A.is_equal, A.mult), join=e)
     e = op("v", lambda: V.tensor_tensor_scan(T.val[:, 16:16 + TC], T.av[:], T.bv[:, 0:TC], T.pcT[:, 32:33], A.add, A.subtract), on=e)
+    c_o = op("v", lambda: V.tensor_scalar(T.off9[:], T.i32c[:], T.pcT[:, 64:65], None, A.add))
     e = op("v", lambda: V.transpose(T.ff[:, 0:TC], T.val[:, 16:16 + TC]), [e])
     op("v", lambda: V.transpose(T.ff[:, TC:2 * TC + 32], T.val[:]), join=e)
     e = op("v", lambda: V.tensor_copy(T.g9[:], T.ff[:, 0:2 * TC + 32].indirect(T.off9[:, 0:7])), [c_o], on=e)
+    c_s = op("v", lambda: V.tensor_copy(T.selo[:], T.pcT[:, 96:98]))
     e_r9 = op("v", lambda: V.tensor_tensor_scan(T.r9[:], T.pmax[:, 0:TC:2], T.g9[:], 0.0, A.add, A.max), on=e)
     e = op("v", lambda: V.tensor_scalar(T.sl[:, 0:14], T.r9[:, 7:112:8], -BIG, None, A.add), on=e_r9)
     e_sc = op("v", lambda: V.tensor_copy(T.win[:, 0:4 * STRIDE].indirect(T.sl[:, 0:14]), T.jv[:]), [c_j], on=e)
 
     sent = [0]
+    own = C * order.index(r)
+    near0 = HALF + (C if me["first"] else 0)
 
     def send_far(stage, dep):
         wait("g", dep)
@@ -238,21 +247,18 @@ def rank_program(g, core, T, topo):
                 sent[0] += len(eng)
             g.remote_dma_fused(tr, local_sem=T.sem.sent)
 
-    def own_first(k, stage):
-        return plan[k]["first"] == (stage == "x")
-
     def send_near(stage, dep):
         wait("g", dep)
         for kind in range(2):
             tr = []
             for k, d in enumerate(me["near"]):
                 eng = _near_masks(topo, core, T.cores[d])[kind][k]
-                a = 3 * C + C * (k + (1 if own_first(r, stage) else 0))
-                b = (0 if own_first(d, stage) else 7 * C) + C * plan[d]["near"].index(r)
+                a = C * k + (near0 - HALF if stage == "x" else 0)
+                b = C * plan[d]["near"].index(r)
                 if kind == 0:
-                    src, dst = _u8(T[stage + "2q"][:, a:a + C]), _u8(T[stage + "2q"][:, b:b + C])
+                    src, dst = _u8(T[stage + "2q"][:, a:a + C]), _u8(T[stage + "2lq"][:, b:b + C])
                 else:
-                    src, dst = T[stage + "2p"][:, a:a + C], T[stage + "2p"][:, b:b + C]
+                    src, dst = T[stage + "2p"][:, a:a + C], T[stage + "2lp"][:, b:b + C]
                 tr.append(RemoteDMATransfer(dst_ids=[_dst(topo, T.cores[d], core)], dma_engine_mask=_mask(eng), remote_sem=T.sem[stage + "near"], src=src, dst=dst))
                 sent[0] += len(eng)
             g.remote_dma_fused(tr, local_sem=T.sem.sent)
@@ -263,10 +269,6 @@ def rank_program(g, core, T, topo):
         mk = _near_masks(topo, T.cores[s], core)
         near_count += len(mk[0][plan[s]["near"].index(r)]) + len(mk[1][plan[s]["near"].index(r)])
 
-    def near_view(stage):
-        a = 0 if own_first(r, stage) else 6 * C
-        return T[stage + "2q"][:, a:a + HALF], T[stage + "2p"][:, a:a + HALF]
-
     q_b = []
     for hf in range(2):
         e = None
@@ -274,14 +276,14 @@ def rank_program(g, core, T, topo):
             c0 = STRIDE * t + STRIDE // 2
             e = op("v", lambda: V.transpose(T.w2[:, 224 * t:224 * t + 96], T.win[:, c0 - 48:c0 + 48]), [e_sc], join=e)
             op("v", lambda: V.transpose(T.w2[:, 224 * t + 96:224 * t + 224], T.win[:, c0 - 64:c0 + 64]), join=e)
-        e_il = op("v", lambda: V.tensor_scalar(T.il[:, 16 * hf:16 * hf + 16], T.w2[:, 448 * hf:448 * hf + 448].indirect(T.selo[:, 0:1]), 0.0, None, A.add), on=e)
+        e_il = op("v", lambda: V.tensor_scalar(T.il[:, 16 * hf:16 * hf + 16], T.w2[:, 448 * hf:448 * hf + 448].indirect(T.selo[:, 0:1]), 0.0, None, A.add), [c_s], on=e)
         lst = T.il[:, 16 * hf:16 * hf + 12]
         lo = 4 * HALF * hf
         gv = gs = None
         for t in range(2):
             gs = op("s", lambda: S.activation(T.xt[:, lo + 2 + t:lo + 4 * HALF:4], T.xpl[:, TC * (2 + t):TC * (3 + t)].indirect(lst), ACT.Copy), [e_il, pl], join=gs)
             gv = op("v", lambda: V.tensor_copy(T.xt[:, lo + t:lo + 4 * HALF:4], T.xpl[:, TC * t:TC * (t + 1)].indirect(lst)), [e_il, pl], join=gv)
-        oq, osc = (T.x1q[:], T.x1p[:]) if hf == 0 else (T.x2q[:, 3 * C:7 * C], T.x2p[:, 3 * C:7 * C])
+        oq, osc = (T.x1q[:], T.x1p[:]) if hf == 0 else (T.x2q[:], T.x2p[:])
         q_b.append(op("v", lambda: V.quantize_mx(oq, osc, T.xt[:, lo:lo + 4 * HALF]), [gs], on=gv))
         (send_far if hf == 0 else send_near)("x", q_b[hf])
 
@@ -292,14 +294,77 @@ def rank_program(g, core, T, topo):
         else:
             c_tab = iota(T.tab[:, C * pos:C * pos + C], [[1, C]], C * order[pos], join=c_tab)
     iota(T.tab[:, N * C:HW], [[0, TC]], -1, join=c_tab)
-    c_d = iota(T.pcol[:], [[0, 2]], 0, 1)
-    iota(T.dc[:], [[16, 16]], N * C, join=c_d)
 
-    q_v = op("v", lambda: V.quantize_mx(T.vq[:], T.vp[:], T.vs[:]), [l_v])
-    e_z = op("v", lambda: V.memset(T.et[:], 0.0))
+    def evacuate(q, out, src, relu, dep, join):
+        if q == "s":
+            return op("s", lambda: S.activation(out, src, ACT.Relu if relu else ACT.Identity, scale=0.0625), [dep], join=join)
+        if relu:
+            return op("v", lambda: V.tensor_scalar(out, src, 0.0, 0.0625, A.max, A.mult), [dep], join=join)
+        return op("v", lambda: V.tensor_scalar(out, src, 0.0625, None, A.mult), [dep], join=join)
+
+    q_z = []
+
+    def expert(s, xc, xp, n, oq, osc):
+        q_h = []
+        for i in range(2):
+            b0 = 4 * ((i + s) % 2)
+            if s > 0 and i == 1:
+                wait("t", q_z[s - 1])
+            k = 2 * s + i
+            lo = 4 * HALF * k
+            done = {"s": None, "v": None}
+            for b in range(4):
+                w = 512 * i + 128 * b
+                m = op("t", lambda: PE.matmul_mx(bank(b0 + b, n), T.aq[:, w:w + 128], T.apl[:, w:w + 128], xc, xp, True, True))
+                q = ("svsv", "sssv")[i][b]
+                done[q] = evacuate(q, T.ht[:, lo + b:lo + 4 * n:4], bank(b0 + b, n), True, m, done[q])
+            q_h.append(op("v", lambda: V.quantize_mx(T.hq[:, HALF * k:HALF * k + n], T.hp[:, HALF * k:HALF * k + n],
+                                                     T.ht[:, lo:lo + 4 * n]), [done["s"]], on=done["v"]))
+        b0 = 4 * (s % 2)
+        lo = 4 * HALF * s
+        wait("t", l_c)
+        done = {"s": None, "v": None}
+        for i in range(2):
+            k = 2 * s + i
+            wait("t", q_h[i])
+            for b in range(4):
+                w = 512 * i + 128 * b
+                call = lambda: PE.matmul_mx(bank(b0 + b, n), T.cq[:, w:w + 128], T.cpl[:, w:w + 128],
+                                            T.hq[:, HALF * k:HALF * k + n], T.hp[:, HALF * k:HALF * k + n], i == 0, i == 1)
+                if i == 0:
+                    call()
+                else:
+                    m = op("t", call)
+                    q = "svsv"[b]
+                    done[q] = evacuate(q, T.zt[:, lo + b:lo + 4 * n:4], bank(b0 + b, n), False, m, done[q])
+        q_z.append(op("v", lambda: V.quantize_mx(oq, osc, T.zt[:, lo:lo + 4 * n]), [done["s"]], on=done["v"]))
+
+    def home(b0, zc, zp, n, at, m_cols, col, whole):
+        out = []
+        for b in range(4):
+            m = op("t", lambda: PE.matmul_mx(bank(b0 + b, n), T.eq[:, 128 * b:128 * b + 128], T.ep[:, 128 * b:128 * b + 128], zc, zp, True, True))
+            out.append(op("v", lambda: V.tensor_tensor(T.hw[:, HW * b + col:HW * b + col + m_cols], bank(b0 + b, m_cols, at),
+                                                       T.xt[:, 4 * col + b:4 * (col + m_cols):4], A.add), [m], join=out[0] if whole and out else None))
+        return out
+
+    a0 = 0 if me["first"] else HALF - 128
+    wait("t", l_a)
+    wait("t", q_b[1])
+    expert(0, T.x2q[:, a0:a0 + 128], T.x2p[:, a0:a0 + 128], 128, T.z0q[:], T.z0p[:])
+    q_e = op("v", lambda: V.quantize_mx(T.eq[:], T.ep[:], T.et[:]), [e_t])
+    PE.wait_ge(T.sem.xfar, far_count)
+    expert(1, T.x1lq[:], T.x1lp[:], HALF, T.z1q[:], T.z1p[:])
+    send_far("z", q_z[1])
+    PE.wait_ge(T.sem.xnear, near_count)
+    expert(2, T.x2lq[:], T.x2lp[:], 3 * C, T.z2q[:], T.z2p[:])
+    send_near("z", q_z[2])
+
     h_x = None
     for t in range(4):
-        h_x = op("v", lambda: V.tensor_copy(T.hw[:, HW * t + N * C:HW * (t + 1)], T.xpl[:, TC * t:TC * (t + 1)]), join=h_x)
+        h_x = op("s", lambda: S.activation(T.hw[:, HW * t + N * C:HW * (t + 1)], T.xpl[:, TC * t:TC * (t + 1)], ACT.Copy), [pl], join=h_x)
+    wait("t", q_e)
+    wait("t", q_z[0])
+    s_own = home(4, T.z0q[:], T.z0p[:], 128, own - HALF - a0, C, own, True)[0]
     n14 = slice(0, 14)
     e = op("v", lambda: V.tensor_scalar(T.d0[:, n14], T.r9[:, 7:112:8], -BIG, None, A.add), [e_r9])
     op("v", lambda: V.tensor_scalar(T.dd[:], T.pidx[:, 0:2], 15, None, A.bitwise_and), join=e)
@@ -316,83 +381,22 @@ def rank_program(g, core, T, topo):
     e = op("v", lambda: V.tensor_tensor(T.da[:, n14], T.d8[:, n14], T.d9[:, n14], A.mult), on=e)
     e = op("v", lambda: V.tensor_tensor(T.db[:, n14], T.da[:, n14], T.d5[:, n14], A.add), on=e)
     e_hl = op("v", lambda: V.tensor_copy(T.hl[:, n14], T.db[:, n14]), on=e)
-    e = None
-    for b in range(4):
-        e = op("v", lambda: V.tensor_scalar(T.et[:, 512 * b + b:512 * (b + 1):4], T.jv[:, 0:128], T.pcol[:, 0:1], None, A.is_equal), [e_z, c_d], join=e)
-    q_e = op("v", lambda: V.quantize_mx(T.eq[:], T.ep[:], T.et[:]), on=e)
+    q_v = op("v", lambda: V.quantize_mx(T.vq[:], T.vp[:], T.vs[:]), [l_v])
     e = op("s", lambda: S.activation(T.olb[:], T.tab[:, 0:HW].indirect(T.hl[:, n14]), ACT.Copy), [e_hl, c_tab])
     stores = op("q", lambda: Q.dma_start(T.ol[:], T.olb[0:128:16, :]), [e], inc=16)
 
-    def evacuate(q, out, src, relu, dep, join):
-        if q == "s":
-            return op("s", lambda: S.activation(out, src, ACT.Relu if relu else ACT.Identity, scale=0.0625), [dep], join=join)
-        if relu:
-            return op("v", lambda: V.tensor_scalar(out, src, 0.0, 0.0625, A.max, A.mult), [dep], join=join)
-        return op("v", lambda: V.tensor_scalar(out, src, 0.0625, None, A.mult), [dep], join=join)
-
-    q_z = []
-    for hf in range(2):
-        xc, xp = (T.x1lq[:], T.x1lp[:]) if hf == 0 else near_view("x")
-        wait("t", l_a)
-        if hf == 0:
-            wait("t", e_r9)
-            PE.wait_ge(T.sem.xfar, far_count)
-        else:
-            wait("t", q_b[1])
-            PE.wait_ge(T.sem.xnear, near_count)
-        q_h = []
-        for i in range(2):
-            b0 = 4 * ((i + hf) % 2)
-            if hf == 1 and i == 1:
-                wait("t", q_z[0])
-            k = 2 * hf + i
-            done = {"s": None, "v": None}
-            for b in range(4):
-                w = 512 * i + 128 * b
-                m = op("t", lambda: PE.matmul_mx(bank(b0 + b, HALF), T.aq[:, w:w + 128], T.apl[:, w:w + 128], xc, xp, True, True))
-                q = ("svsv", "sssv")[i][b]
-                done[q] = evacuate(q, T.ht[:, 4 * HALF * k + b:4 * HALF * (k + 1):4], bank(b0 + b, HALF), True, m, done[q])
-            q_h.append(op("v", lambda: V.quantize_mx(T.hq[:, HALF * k:HALF * (k + 1)], T.hp[:, HALF * k:HALF * (k + 1)],
-                                                     T.ht[:, 4 * HALF * k:4 * HALF * (k + 1)]), [done["s"]], on=done["v"]))
-        b0 = 4 * hf
-        wait("t", l_c)
-        done = {"s": None, "v": None}
-        for i in range(2):
-            k = 2 * hf + i
-            wait("t", q_h[i])
-            for b in range(4):
-                w = 512 * i + 128 * b
-                call = lambda: PE.matmul_mx(bank(b0 + b, HALF), T.cq[:, w:w + 128], T.cpl[:, w:w + 128],
-                                            T.hq[:, HALF * k:HALF * (k + 1)], T.hp[:, HALF * k:HALF * (k + 1)], i == 0, i == 1)
-                if i == 0:
-                    call()
-                else:
-                    m = op("t", call)
-                    q = "svsv"[b]
-                    done[q] = evacuate(q, T.zt[:, 4 * HALF * hf + b:4 * HALF * (hf + 1):4], bank(b0 + b, HALF), False, m, done[q])
-        oq, osc = (T.z1q[:], T.z1p[:]) if hf == 0 else (T.z2q[:, 3 * C:7 * C], T.z2p[:, 3 * C:7 * C])
-        q_z.append(op("v", lambda: V.quantize_mx(oq, osc, T.zt[:, 4 * HALF * hf:4 * HALF * (hf + 1)]), [done["s"]], on=done["v"]))
-        (send_far if hf == 0 else send_near)("z", q_z[hf])
-
-    added = {}
-    wait("t", q_e)
-    for hf in range(2):
-        zc, zp = (T.z1lq[:], T.z1lp[:]) if hf == 0 else near_view("z")
-        if hf == 0:
-            PE.wait_ge(T.sem.zfar, far_count)
-        else:
-            wait("t", q_z[1])
-            PE.wait_ge(T.sem.znear, near_count)
-        for b in range(4):
-            m = op("t", lambda: PE.matmul_mx(bank(4 * hf + b, HALF), T.eq[:, 128 * b:128 * b + 128], T.ep[:, 128 * b:128 * b + 128], zc, zp, True, True))
-            lo = 4 * HALF * hf
-            added[(hf, b)] = op("v", lambda: V.tensor_tensor(T.hw[:, HW * b + HALF * hf:HW * b + HALF * (hf + 1)], bank(4 * hf + b, HALF),
-                                                             T.xt[:, lo + b:lo + 4 * HALF:4], A.add), [m], join=added.get((0, 0)) if hf == 0 else None)
+    wait("t", q_z[2])
+    PE.wait_ge(T.sem.zfar, far_count)
+    s_far = home(0, T.z1lq[:], T.z1lp[:], HALF, 0, HALF, 0, True)[0]
+    wait("t", s_own)
+    PE.wait_ge(T.sem.znear, near_count)
+    s_near = home(4, T.z2lq[:], T.z2lp[:], 3 * C, 0, 3 * C, near0, False)
     gs = None
-    for b in range(3):
-        gs = op("s", lambda: S.activation(T.yt[:, b:4 * TC:4], T.hw[:, HW * b:HW * (b + 1)].indirect(T.hl[:, n14]), ACT.Copy),
-                [h_x, added[(0, 0)], added[(1, b)]], join=gs)
-    gv = op("v", lambda: V.tensor_copy(T.yt[:, 3:4 * TC:4], T.hw[:, HW * 3:HW * 4].indirect(T.hl[:, n14])), [h_x, added[(0, 0)], e_hl], on=added[(1, 3)])
+    for b, k in ((0, 14), (1, 14), (2, 8)):
+        gs = op("s", lambda: S.activation(T.yt[:, b:64 * k:4], T.hw[:, HW * b:HW * (b + 1)].indirect(T.hl[:, 0:k]), ACT.Copy),
+                [h_x, s_own, s_far, s_near[b]], join=gs)
+    gv = op("v", lambda: V.tensor_copy(T.yt[:, 512 + 2:4 * TC:4], T.hw[:, HW * 2:HW * 3].indirect(T.hl[:, 8:14])), [h_x, s_own, s_far, e_hl, s_near[2]])
+    op("v", lambda: V.tensor_copy(T.yt[:, 3:4 * TC:4], T.hw[:, HW * 3:HW * 4].indirect(T.hl[:, n14])), [s_near[3]], join=gv)
     q_y = op("v", lambda: V.quantize_mx(T.yq[:], T.yp[:], T.yt[:]), [gs], on=gv)
     m = op("t", lambda: PE.matmul_mx(bank(0, TC), T.vq[:], T.vp[:], T.yq[:], T.yp[:], True, True), [q_v, q_y])
     op("q", lambda: Q.dma_start(T.oc[:], _u8(T.yq[:])), [q_y], join=stores, inc=16)

@@ -2,11 +2,13 @@ from concourse.bass import DstId, RemoteDMATransfer
 from concourse.mybir import dt, AluOpType, ActivationFunctionType
 
 N, TC, C = 8, 224, 48
-HALF = 4 * C
-BIG = 4096.0
-STRIDE = 512
+FAR, NEAR = 4 * C, 3 * C
+PAD = 128 - C
+SEG = TC // 2
+RUN, LANE = 256, 2048
 HW = 8 * C + TC
 F8, U8, U16, BF, F32, I32 = "float8_e4m3fn_x4", "uint8", "uint16", "bfloat16", "float32", "int32"
+BY = ["svsv", "sssv", "svsv", "svsv", "sssv", "sssv", "svsv", "sssv", "svsv"]
 
 
 def _sb(n, d):
@@ -16,29 +18,27 @@ def _sb(n, d):
 SCRATCH = {
     "ps": ("psum", [128, 4096], F32),
     "xs": _sb(4 * TC, BF), "us": _sb(512, BF), "vs": _sb(512, BF),
-    "xq": _sb(TC, F8), "xp": _sb(TC, U8), "uq": _sb(128, F8), "up": _sb(128, U8),
+    "xq": _sb(256, F8), "xp": _sb(256, U8), "uq": _sb(128, F8), "up": _sb(128, U8),
     "uq2": _sb(128, F8), "up2": _sb(128, U8), "vq": _sb(128, F8), "vp": _sb(128, U8),
     "aq": _sb(1024, F8), "apl": _sb(1024, U8), "cq": _sb(1024, F8), "cpl": _sb(1024, U8),
     "pidx": _sb(8, I32), "i16": _sb(8, I32), "t0": _sb(8, I32), "t1": _sb(8, I32), "uoff": _sb(8, U16),
-    "pc": _sb(128, F32), "pcT": _sb(128, F32), "i32c": _sb(8, F32), "off9": _sb(8, U16), "selo": _sb(2, U16),
-    "jv": _sb(TC, BF), "pmax": _sb(TC, F32), "ptwo": _sb(TC, BF),
-    "pt": _sb(TC, F32), "rm": _sb(TC, F32), "hit": _sb(TC, BF), "st": _sb(TC, BF), "stT": _sb(TC, BF),
-    "av": _sb(TC, F32), "bv": _sb(TC + 8, BF), "val": _sb(TC + 32, F32), "ff": _sb(2 * TC + 32, F32),
-    "g9": _sb(112, F32), "r9": _sb(112, F32), "sl": _sb(16, U16),
-    "win": _sb(4 * STRIDE, BF), "w2": _sb(4 * 224, BF), "il": _sb(32, U16),
-    "xpl": _sb(4 * TC, BF), "xt": _sb(8 * HALF, BF),
-    "x1q": _sb(HALF, F8), "x1p": _sb(HALF, U8), "x1lq": _sb(HALF, F8), "x1lp": _sb(HALF, U8),
-    "x2q": _sb(HALF, F8), "x2p": _sb(HALF, U8), "x2lq": _sb(3 * C, F8), "x2lp": _sb(3 * C, U8),
+    "pc": _sb(128, F32), "pcT": _sb(128, F32), "mlist": _sb(8, U16), "glist": _sb(2, U16),
+    "jv": _sb(TC, BF), "pmax": _sb(SEG, F32), "crow": _sb(TC, BF), "im": _sb(C, BF), "diag": _sb(C, BF),
+    "pt": _sb(TC, F32), "rm": _sb(152, F32), "rn": _sb(SEG, F32), "ee": _sb(SEG + 8, BF), "gs": _sb(TC, BF), "gT": _sb(TC, BF),
+    "val": _sb(TC, F32), "vT": _sb(TC, F32), "tw": _sb(32 + 512, F32), "tu": _sb(64, F32), "sl": _sb(16, U16),
+    "win": _sb(N * LANE, BF), "ex": _sb(N * C, BF), "il": _sb(32, U16),
+    "xpl": _sb(4 * TC, BF), "xt": _sb(4 * N * C, BF),
+    "x1q": _sb(FAR, F8), "x1p": _sb(FAR, U8), "x1lq": _sb(FAR, F8), "x1lp": _sb(FAR, U8),
+    "x2q": _sb(FAR, F8), "x2p": _sb(FAR, U8), "x2lq": _sb(NEAR, F8), "x2lp": _sb(NEAR, U8),
     "z0q": _sb(128, F8), "z0p": _sb(128, U8),
-    "z1q": _sb(HALF, F8), "z1p": _sb(HALF, U8), "z1lq": _sb(HALF, F8), "z1lp": _sb(HALF, U8),
-    "z2q": _sb(3 * C, F8), "z2p": _sb(3 * C, U8), "z2lq": _sb(3 * C, F8), "z2lp": _sb(3 * C, U8),
+    "z1q": _sb(FAR, F8), "z1p": _sb(FAR, U8), "z1lq": _sb(FAR, F8), "z1lp": _sb(FAR, U8),
+    "z2q": _sb(NEAR, F8), "z2p": _sb(NEAR, U8), "z2lq": _sb(NEAR, F8), "z2lp": _sb(NEAR, U8),
     "rxq": _sb(2 * C, F8), "rxp": _sb(2 * C, U8), "rzq": _sb(2 * C, F8), "rzp": _sb(2 * C, U8),
-    "ht": _sb(24 * HALF, BF), "hq": _sb(6 * HALF, F8), "hp": _sb(6 * HALF, U8), "zt": _sb(12 * HALF, BF),
-    "eb": _sb(516, BF), "et": _sb(2048, BF), "eq": _sb(512, F8), "ep": _sb(512, U8),
+    "ht": _sb(24 * FAR, BF), "hq": _sb(6 * FAR, F8), "hp": _sb(6 * FAR, U8), "zt": _sb(12 * FAR, BF),
+    "eb": _sb(516, BF), "eq": _sb(512, F8), "ep": _sb(512, U8),
     "hw": _sb(4 * HW, BF), "tab": _sb(HW, F32), "olb": _sb(TC, F32),
     "d0": _sb(16, I32), "d1": _sb(16, I32), "d2": _sb(16, I32), "d3": _sb(16, F32), "d4": _sb(16, F32),
-    "d5": _sb(16, F32), "d6": _sb(16, F32), "d7": _sb(16, F32), "d8": _sb(16, F32), "d9": _sb(16, F32),
-    "da": _sb(16, F32), "db": _sb(16, F32), "dc": _sb(16, I32), "dd": _sb(2, I32), "de": _sb(2, F32), "hl": _sb(16, U16),
+    "d5": _sb(16, F32), "d6": _sb(16, F32), "d7": _sb(16, F32), "d8": _sb(16, F32), "dc": _sb(16, F32), "hl": _sb(16, U16),
     "yt": _sb(4 * TC, BF), "yq": _sb(TC, F8), "yp": _sb(TC, U8), "yo": _sb(TC, F32),
 }
 SEMAPHORES = ["sent", "xfar", "xnear", "zfar", "znear", "rx", "rz"] + ["e%d" % k for k in range(143)]
@@ -56,21 +56,13 @@ def _plan(T, topo):
     plan = []
     for r in range(N):
         far = [d for d in range(N) if d != r and not topo.may_write(cores[r], cores[d])]
-        near = [d for d in range(N) if d not in far]
-        assert len(far) == 4 and all(s[k + 2] == s[k] + N // 2 for s in (far, near) for k in range(2))
-        fp = [[far[0], far[2]], [far[1], far[3]]]
-        if near.index(r) % 2:
-            fp = fp[::-1]
-        npair = [[near[0], near[2]], [near[1], near[3]]]
-        mine = [p for p in npair if r in p][0]
-        other = [p for p in npair if r not in p][0]
-        first = mine[0] == r
-        order = fp[0] + fp[1] + (mine + other if first else other + mine)
+        near = [d for d in range(N) if d not in far and d != r]
+        assert len(far) == 4
+        far = far[r // 2:] + far[:r // 2]
         able = [c for c in topo.cores_of(cores[r]) if c not in cores and all(topo.may_write(c, cores[d]) for d in far)]
         same = [c for c in able if topo.die(c) == topo.die(cores[r])]
         across = [c for c in able if topo.die(c) != topo.die(cores[r])]
-        plan.append({"order": order, "first": first, "codes": [same[0], across[0]], "scales": [same[1], across[1]],
-                     "near": [d for d in order[4:] if d != r]})
+        plan.append({"order": far + near + [r], "codes": [same[0], across[0]], "scales": [same[1], across[1]], "near": near})
     return plan
 
 
@@ -78,6 +70,10 @@ def _near_masks(topo, src, dst):
     e = topo.engines(src, dst)
     h, q = len(e) // 2, len(e) // 4
     return [e[:h], e[h:h + q], e[h + q:]], [e[:q], e[q:h], e[h:]]
+
+
+def _hand_engines(topo, plan, T, r, stage, kind, t):
+    return topo.engines(T.cores[r], plan[r][kind][t])[t::2]
 
 
 def _dst(topo, dst, src):
@@ -94,10 +90,9 @@ def _helper(g, core, T, topo, plan):
         for kind in ("codes", "scales"):
             if core in plan[r][kind]:
                 t = plan[r][kind].index(core)
-                came = len(topo.engines(T.cores[r], core)) // 2
                 total = 0
                 for stage in ("x", "z"):
-                    g.wait_ge(T.sem["r" + stage], came)
+                    g.wait_ge(T.sem["r" + stage], len(_hand_engines(topo, plan, T, r, stage, kind, t)))
                     tr = []
                     for k in range(2):
                         d = plan[r]["order"][2 * t + k]
@@ -158,79 +153,113 @@ def rank_program(g, core, T, topo):
             return op("g", lambda: g.iota(out, pattern, base, cm), deps, join=join)
         return op("g", lambda: g.iota(out, pattern, base, cm, allow_small_or_imprecise_dtypes=True), deps, join=join)
 
+    def fill(view, value, join=None):
+        return op("v", lambda: V.memset(view, value), join=join)
+
+    def run(d):
+        return LANE * (N - 1 - d) + RUN * order.index(d) + 16
+
     l_u = op("q", lambda: Q.dma_start(T.us[:], T.u[:]), inc=16)
-    l_x = op("q", lambda: Q.dma_start(T.xs[:], T.x[:]), inc=16)
+    l_xa = op("q", lambda: Q.dma_start(T.xs[:, 0:512], T.x[:, 0:512]), inc=16)
+    l_xb = op("q", lambda: Q.dma_start(T.xs[:, 512:4 * TC], T.x[:, 512:4 * TC]), inc=16)
     l_a = op("q", lambda: Q.dma_start(_u8(T.aq[:]), T.ac[:]), inc=16)
     op("q", lambda: Q.dma_start(T.apl[:], T.ap[:]), join=l_a, inc=16)
     l_c = op("q", lambda: Q.dma_start(_u8(T.cq[:]), T.cc[:]), inc=16)
     op("q", lambda: Q.dma_start(T.cpl[:], T.cp[:]), join=l_c, inc=16)
-    l_v = op("q", lambda: Q.dma_start(T.vs[:], T.v[:]), inc=16)
 
-    m_e = op("v", lambda: V.memset(T.eb[:], 1.0))
     c_p = iota(T.pidx[:], [[0, 8]], 0, 1)
     iota(T.i16[:], [[16, 8]], 0, join=c_p)
-    c_pc = iota(T.pc[:, 0:32], [[0, 4], [2, 2], [0, 4]], int(BIG) - 1)
-    for d in range(N // 2):
-        iota(T.pc[:, 32 + d:64:4], [[0, 4], [-1, 2]], STRIDE * (order.index(d) // 2) + STRIDE // 2, join=c_pc)
-    for k, add in enumerate((8, TC + 32, TC + 8, 0)):
-        iota(T.pc[:, 64 + 8 * k:72 + 8 * k], [[1, 8]], 8 * k + add, join=c_pc)
+    c_pc = None
     for h in range(2):
         for par in range(2):
-            base = 16 * h + (0 if par == h else 96 + 32 * (1 - h))
-            iota(T.pc[:, 96 + 16 * h + par:96 + 16 * h + 12:2], [[224, 2], [32, 3]], base, join=c_pc)
-    iota(T.i32c[:], [[32, 8]], 0, join=c_pc)
-    c_e = op("g", lambda: g.affine_select(T.eb[:], T.eb[:], [[1, 516]], A.is_equal, 0.0, -3, -4), [m_e])
+            view = T.pc[:, 64 + 16 * h + par:80 + 16 * h:2]
+            c_pc = iota(view, [[16, 8]], 32 + 8 * h + 7, join=c_pc) if par == h else iota(view, [[1, 8]], 0, join=c_pc)
+    iota(T.pc[:, 96:128], [[0, 2], [1, 16]], 0, join=c_pc)
     c_j = iota(T.jv[:], [[1, TC]], 0)
+    iota(T.im[:], [[0, 3], [1, 16]], 0, join=c_j)
     c_d = iota(T.dc[:], [[16, 16]], N * C)
+    c_w = None
+    for d in order:
+        c_w = iota(T.win[:, run(d):run(d) + C], [[0, C]], TC - 1, join=c_w)
+    c_e = iota(T.eb[:], [[0, 516]], 1)
+    c_e = op("g", lambda: g.affine_select(T.eb[:], T.eb[:], [[1, 516]], A.is_equal, 0.0, -3, -4), on=c_e)
 
-    m0 = op("v", lambda: V.memset(T.pmax[:], 0.0))
-    op("v", lambda: V.memset(T.ptwo[:], 2.0), join=m0)
-    m1 = op("v", lambda: V.memset(T.pc[:, 108:112], 0.0))
-    op("v", lambda: V.memset(T.pc[:, 124:128], 0.0), join=m1)
-    op("v", lambda: V.memset(T.val[:, 0:16], 0.0), join=m1)
-    op("v", lambda: V.memset(T.val[:, 16 + TC:32 + TC], 0.0), join=m1)
-    op("v", lambda: V.memset(T.bv[:, 0:1], 0.0), join=m1)
-    for t in range(4):
-        op("v", lambda: V.memset(T.win[:, STRIDE * t + 192:STRIDE * t + 320], 0.0), join=m1)
-    op("v", lambda: V.memset(T.pmax[:, 0:TC:16], -1e29), [m0], join=m1)
-    op("v", lambda: V.memset(T.ptwo[:, 8:TC:16], 0.0), join=m1)
-    e = op("v", lambda: V.tensor_scalar(T.t0[:], T.pidx[:], 7, None, A.bitwise_and), [c_p])
+    m0 = fill(T.pmax[:], 0.0)
+    m_pc = fill(T.pc[:, 7:32:8], 64.0)
+    for k in range(4):
+        fill(T.pc[:, 8 * k:8 * k + 7], 8.0 * (k % 2) + 7.0, m_pc)
+    for d in range(N):
+        fill(T.pc[:, 32 + 2 * d:64:16], run(d) - 1.0, m_pc)
+    fill(T.pc[:, 33:64:2], 0.0, m_pc)
+    e = op("v", lambda: V.tensor_scalar(T.t0[:], T.pidx[:], 1, 7, A.logical_shift_right, A.bitwise_and), [c_p])
+    m1 = fill(T.rm[:, 64:72], 1e29)
+    fill(T.rm[:, 128:152], 1e29, m1)
+    fill(T.ee[:, 0:1], 0.0, m1)
     e = op("v", lambda: V.tensor_tensor(T.t1[:], T.t0[:], T.i16[:], A.add), on=e)
+    fill(T.gs[:, 1:TC:2], 0.0, m1)
+    fill(T.tw[:, 32 + SEG + 7:544:8], 0.0, m1)
     c_uo = op("v", lambda: V.tensor_copy(T.uoff[:], T.t1[:]), on=e)
+    op("v", lambda: V.memset(T.pmax[:, 0:SEG:8], -1e29), [m0], join=m1)
+    c_t = op("v", lambda: V.transpose(T.pcT[:], T.pc[:]), [c_pc, m_pc])
 
     q_u = op("v", lambda: V.quantize_mx(T.uq[:], T.up[:], T.us[:]), [l_u])
+    c_l = op("v", lambda: V.tensor_scalar(T.mlist[:], T.i16[:], T.pcT[:, 0:1], 64.0, A.add, A.min), [c_t])
     k_u = op("v", lambda: V.tensor_copy(T.uq2[:, 0:128].bitcast(dt.uint32), T.uq[:, 0:128].bitcast(dt.uint32).indirect(T.uoff[:, 0:8])), [q_u, c_uo])
     k_s = op("s", lambda: S.activation(T.up2[:, 0:128], T.up[:, 0:128].indirect(T.uoff[:, 0:8]), ACT.Copy), [q_u, c_uo])
-    q_x = op("v", lambda: V.quantize_mx(T.xq[:], T.xp[:], T.xs[:]), [l_x])
-    m_p = op("t", lambda: PE.matmul_mx(bank(0, TC), T.uq2[:], T.up2[:], T.xq[:], T.xp[:], True, True), [k_u, k_s, q_x])
+    q_xa = op("v", lambda: V.quantize_mx(T.xq[:, 0:128], T.xp[:, 0:128], T.xs[:, 0:512]), [l_xa])
+    m_a = op("t", lambda: PE.matmul_mx(bank(0, 128), T.uq2[:], T.up2[:], T.xq[:, 0:128], T.xp[:, 0:128], True, True), [k_u, k_s, q_xa])
+    op("v", lambda: V.tensor_scalar(T.crow[:], T.jv[:], run(N - 1) - 1.0, T.pcT[:, 32:33], A.add, A.is_ge), [c_j], join=c_l)
+    q_xb = op("v", lambda: V.quantize_mx(T.xq[:, 128:256], T.xp[:, 128:256], T.xs[:, 4 * TC - 512:4 * TC]), [l_xb])
+    m_b = op("t", lambda: PE.matmul_mx(bank(1, 128), T.uq2[:], T.up2[:], T.xq[:, 128:256], T.xp[:, 128:256], True, True), [q_xb])
     pl = None
     for t in range(4):
-        pl = op("s", lambda: S.activation(T.xpl[:, TC * t:TC * t + TC], T.xs[:, t:4 * TC:4], ACT.Copy), [l_x], join=pl)
-    e_t = None
-    for b in range(4):
-        e_t = op("s", lambda: S.activation(T.et[:, 512 * b:512 * (b + 1)], T.eb[:, 3 - b:515 - b], ACT.Copy), [c_e], join=e_t)
+        pl = op("s", lambda: S.activation(T.xpl[:, TC * t:TC * t + TC], T.xs[:, t:4 * TC:4], ACT.Copy), [l_xa, l_xb], join=pl)
+    h_x = None
+    for t in range(4):
+        h_x = op("s", lambda: S.activation(T.hw[:, HW * t + N * C:HW * (t + 1)], T.xs[:, t:4 * TC:4], ACT.Copy), join=h_x)
+    pad = None
+    for tile in (T.ht[:, 0:4 * PAD], T.ht[:, 4 * FAR:4 * (FAR + PAD)], T.zt[:, 0:4 * PAD]):
+        pad = op("s", lambda: S.activation(tile, T.xs[:, 0:4 * PAD], ACT.Identity, scale=0.0), join=pad)
 
-    e = op("v", lambda: V.transpose(T.pt[:], bank(0, TC)), [m_p, m1])
-    e = op("v", lambda: V.tensor_tensor_scan(T.rm[:], T.pmax[:], T.pt[:], 0.0, A.add, A.max), on=e)
-    e = op("v", lambda: V.tensor_tensor(T.hit[:], T.pt[:], T.rm[:], A.is_equal), on=e)
-    e = op("v", lambda: V.tensor_tensor_scan(T.st[:], T.ptwo[:], T.hit[:], 0.0, A.mult, A.add), on=e)
-    e = op("v", lambda: V.transpose(T.stT[:], T.st[:]), on=e)
-    op("v", lambda: V.transpose(T.pcT[:], T.pc[:]), [c_pc], join=e)
-    e = op("v", lambda: V.tensor_scalar(T.av[:], T.stT[:], 1.0, T.pcT[:, 0:1], A.is_equal, A.mult), [e])
-    op("v", lambda: V.tensor_scalar(T.bv[:, 1:TC + 1], T.stT[:], 1.0, BIG, A.is_equal, A.mult), join=e)
-    e = op("v", lambda: V.tensor_tensor_scan(T.val[:, 16:16 + TC], T.av[:], T.bv[:, 0:TC], T.pcT[:, 32:33], A.add, A.subtract), on=e)
-    c_o = op("v", lambda: V.tensor_scalar(T.off9[:], T.i32c[:], T.pcT[:, 64:65], None, A.add))
-    e = op("v", lambda: V.transpose(T.ff[:, 0:TC], T.val[:, 16:16 + TC]), [e])
-    op("v", lambda: V.transpose(T.ff[:, TC:2 * TC + 32], T.val[:]), join=e)
-    e = op("v", lambda: V.tensor_copy(T.g9[:], T.ff[:, 0:2 * TC + 32].indirect(T.off9[:, 0:7])), [c_o], on=e)
-    c_s = op("v", lambda: V.tensor_copy(T.selo[:], T.pcT[:, 96:98]))
-    e_r9 = op("v", lambda: V.tensor_tensor_scan(T.r9[:], T.pmax[:, 0:TC:2], T.g9[:], 0.0, A.add, A.max), on=e)
-    e = op("v", lambda: V.tensor_scalar(T.sl[:, 0:14], T.r9[:, 7:112:8], -BIG, None, A.add), on=e_r9)
-    e_sc = op("v", lambda: V.tensor_copy(T.win[:, 0:4 * STRIDE].indirect(T.sl[:, 0:14]), T.jv[:]), [c_j], on=e)
+    cols, segs, wins = ((0, 128), (128, TC)), ((0, 64), (64, SEG)), (0, 80)
+
+    def step(k, h, deps=(), on=None):
+        (c0, c1), (s0, s1), w = cols[h], segs[h], wins[h]
+        if k == 0:
+            return op("v", lambda: V.transpose(T.pt[:, c0:c1], bank(h, c1 - c0, 128 - (c1 - c0))), deps, on=on)
+        if k == 1:
+            e = op("v", lambda: V.tensor_tensor_scan(T.rm[:, w:w + s1 - s0], T.pmax[:, s0:s1], T.pt[:, c0:c1:2], 0.0, A.add, A.max), deps, on=on)
+            return op("v", lambda: V.tensor_tensor_scan(T.rn[:, s0:s1], T.pmax[:, s0:s1], T.pt[:, c0:c1:2], 0.0, A.add, A.max), join=e)
+        if k == 2:
+            return op("v", lambda: V.tensor_tensor(T.ee[:, s0 + 1:s1 + 1], T.rm[:, w:w + 72].indirect(T.mlist[:, 0:(s1 - s0) // 16]), T.rn[:, s0:s1], A.is_equal), deps, on=on)
+        if k == 3:
+            return op("v", lambda: V.tensor_tensor(T.gs[:, c0:c1:2], T.ee[:, s0 + 1:s1 + 1], T.ee[:, s0:s1], A.subtract), deps, on=on)
+        if k == 4:
+            return op("v", lambda: V.transpose(T.gT[:, c0:c1], T.gs[:, c0:c1]), deps, on=on)
+        if k == 5:
+            first = T.val[:, c0 - 1:c0] if h else T.pcT[:, 32:33]
+            return op("v", lambda: V.tensor_tensor_scan(T.val[:, c0:c1], T.crow[:, c0:c1], T.gT[:, c0:c1], first, A.add, A.add), deps, on=on)
+        if k == 6:
+            return op("v", lambda: V.transpose(T.vT[:, c0:c1], T.val[:, c0:c1]), deps, on=on)
+        return op("v", lambda: V.tensor_tensor_scan(T.tw[:, 32 + s0:32 + s1], T.ee[:, s0:s1], T.vT[:, c0:c1:2], 0.0, A.mult, A.max), deps, on=on)
+
+    ea = step(0, 0, [m_a, m1])
+    op("v", lambda: V.tensor_scalar(T.glist[:], T.pcT[:, 64:66], 31.0 + SEG, None, A.min), join=c_l)
+    op("v", lambda: V.tensor_scalar(T.diag[:], T.im[:], T.pcT[:, 96:97], 512.0, A.is_equal, A.mult), join=c_l)
+    ea = step(1, 0, on=ea)
+    eb = step(0, 1, [m_b])
+    for k in range(2, 8):
+        ea = step(k, 0, [c_l], on=ea)
+        eb = step(k - 1, 1, on=eb)
+    e = step(7, 1, on=eb)
+    wait("v", ea)
+    e = op("v", lambda: V.transpose(T.tu[:, 0:32], T.tw[:, 39:544:16]), on=e)
+    op("v", lambda: V.transpose(T.tu[:, 32:64], T.tw[:, 47:544:16]), join=e)
+    e = op("v", lambda: V.transpose(T.tw[:, 0:32], T.tu[:, 16:48]), on=e)
+    e_sl = op("v", lambda: V.tensor_scalar(T.sl[:], T.tw[:, 0:32 + SEG].indirect(T.glist[:, 0:1]), 0.0, None, A.add), on=e)
+    e_sc = op("v", lambda: V.tensor_copy(T.win[:, 0:N * LANE].indirect(T.sl[:, 0:14]), T.jv[:]), [c_w, e_sl])
 
     sent = [0]
-    own = C * order.index(r)
-    near0 = HALF + (C if me["first"] else 0)
 
     def send_far(stage, dep):
         wait("g", dep)
@@ -238,7 +267,7 @@ def rank_program(g, core, T, topo):
             tr = []
             for t in range(2):
                 c = me[kind][t]
-                eng = topo.engines(core, c)[t::2]
+                eng = _hand_engines(topo, plan, T, r, stage, kind, t)
                 if kind == "codes":
                     src, dst = _u8(T[stage + "1q"][:, 2 * C * t:2 * C * (t + 1)]), _u8(T["r%sq" % stage][:])
                 else:
@@ -253,7 +282,7 @@ def rank_program(g, core, T, topo):
             tr = []
             for k, d in enumerate(me["near"]):
                 eng = _near_masks(topo, core, T.cores[d])[kind][k]
-                a = C * k + (near0 - HALF if stage == "x" else 0)
+                a = C * k
                 b = C * plan[d]["near"].index(r)
                 if kind == 0:
                     src, dst = _u8(T[stage + "2q"][:, a:a + C]), _u8(T[stage + "2lq"][:, b:b + C])
@@ -269,135 +298,155 @@ def rank_program(g, core, T, topo):
         mk = _near_masks(topo, T.cores[s], core)
         near_count += len(mk[0][plan[s]["near"].index(r)]) + len(mk[1][plan[s]["near"].index(r)])
 
-    q_b = []
-    for hf in range(2):
-        e = None
-        for t in (2 * hf, 2 * hf + 1):
-            c0 = STRIDE * t + STRIDE // 2
-            e = op("v", lambda: V.transpose(T.w2[:, 224 * t:224 * t + 96], T.win[:, c0 - 48:c0 + 48]), [e_sc], join=e)
-            op("v", lambda: V.transpose(T.w2[:, 224 * t + 96:224 * t + 224], T.win[:, c0 - 64:c0 + 64]), join=e)
-        e_il = op("v", lambda: V.tensor_scalar(T.il[:, 16 * hf:16 * hf + 16], T.w2[:, 448 * hf:448 * hf + 448].indirect(T.selo[:, 0:1]), 0.0, None, A.add), [c_s], on=e)
-        lst = T.il[:, 16 * hf:16 * hf + 12]
-        lo = 4 * HALF * hf
-        gv = gs = None
-        for t in range(2):
-            gs = op("s", lambda: S.activation(T.xt[:, lo + 2 + t:lo + 4 * HALF:4], T.xpl[:, TC * (2 + t):TC * (3 + t)].indirect(lst), ACT.Copy), [e_il, pl], join=gs)
-            gv = op("v", lambda: V.tensor_copy(T.xt[:, lo + t:lo + 4 * HALF:4], T.xpl[:, TC * t:TC * (t + 1)].indirect(lst)), [e_il, pl], join=gv)
-        oq, osc = (T.x1q[:], T.x1p[:]) if hf == 0 else (T.x2q[:], T.x2p[:])
-        q_b.append(op("v", lambda: V.quantize_mx(oq, osc, T.xt[:, lo:lo + 4 * HALF]), [gs], on=gv))
-        (send_far if hf == 0 else send_near)("x", q_b[hf])
+    def pick(b, join=None):
+        w = run(order[b])
+        return op("v", lambda: V.tensor_tensor_scan(T.ex[:, C * b:C * b + C], T.diag[:], T.win[:, w:w + C], 0.0, A.add, A.min), [e_sc], join=join)
+
+    def listed(hf, e):
+        return op("v", lambda: V.tensor_copy(T.il[:, 12 * hf:12 * hf + 12], T.ex[:, FAR * hf + 15:FAR * (hf + 1):16]), on=e)
+
+    def gather(q, hf, t, e, join):
+        out, src = T.xt[:, 4 * FAR * hf + t:4 * FAR * (hf + 1):4], T.xpl[:, TC * t:TC * (t + 1)].indirect(T.il[:, 12 * hf:12 * hf + 12])
+        if q == "s":
+            return op("s", lambda: S.activation(out, src, ACT.Copy), [e, pl], join=join)
+        return op("v", lambda: V.tensor_copy(out, src), [e, pl], join=join)
+
+    ef = en = None
+    for b in range(4):
+        ef = pick(b, ef)
+    for b in (4, 5):
+        en = pick(b, en)
+    ef = listed(0, ef)
+    for b in (6, 7):
+        en = pick(b, en)
+    gv = gather("v", 0, 1, ef, gather("v", 0, 0, ef, None))
+    gs = gather("s", 0, 3, ef, gather("s", 0, 2, ef, None))
+    en = listed(1, en)
+    send_far("x", op("v", lambda: V.quantize_mx(T.x1q[:], T.x1p[:], T.xt[:, 0:4 * FAR]), [gs], on=gv))
+    gv = gather("v", 1, 1, en, gather("v", 1, 0, en, None))
+    gs = gather("s", 1, 3, en, gather("s", 1, 2, en, None))
+    q_own = op("v", lambda: V.quantize_mx(T.x2q[:], T.x2p[:], T.xt[:, 4 * FAR:8 * FAR]), [gs], on=gv)
+    send_near("x", q_own)
 
     c_tab = None
     for pos in range(N):
-        if pos % 2 == 0:
-            c_tab = iota(T.tab[:, C * pos:C * pos + C], [[-1, C]], C * order[pos] + C - 1, join=c_tab)
-        else:
-            c_tab = iota(T.tab[:, C * pos:C * pos + C], [[1, C]], C * order[pos], join=c_tab)
+        c_tab = iota(T.tab[:, C * pos:C * pos + C], [[1, C]], C * order[pos], join=c_tab)
     iota(T.tab[:, N * C:HW], [[0, TC]], -1, join=c_tab)
 
-    def evacuate(q, out, src, relu, dep, join):
+    def evacuate(q, out, src, relu, dep, on):
         if q == "s":
-            return op("s", lambda: S.activation(out, src, ACT.Relu if relu else ACT.Identity, scale=0.0625), [dep], join=join)
+            return op("s", lambda: S.activation(out, src, ACT.Relu if relu else ACT.Identity, scale=0.0625), [dep], join=on)
         if relu:
-            return op("v", lambda: V.tensor_scalar(out, src, 0.0, 0.0625, A.max, A.mult), [dep], join=join)
-        return op("v", lambda: V.tensor_scalar(out, src, 0.0625, None, A.mult), [dep], join=join)
+            return op("v", lambda: V.tensor_scalar(out, src, 0.0, 0.0625, A.max, A.mult), [dep], join=on)
+        return op("v", lambda: V.tensor_scalar(out, src, 0.0625, None, A.mult), [dep], join=on)
 
-    q_z = []
+    free = {0: [], 4: []}
 
-    def expert(s, xc, xp, n, oq, osc):
-        q_h = []
-        for i in range(2):
-            b0 = 4 * ((i + s) % 2)
-            if s > 0 and i == 1:
-                wait("t", q_z[s - 1])
-            k = 2 * s + i
-            lo = 4 * HALF * k
-            done = {"s": None, "v": None}
-            for b in range(4):
-                w = 512 * i + 128 * b
-                m = op("t", lambda: PE.matmul_mx(bank(b0 + b, n), T.aq[:, w:w + 128], T.apl[:, w:w + 128], xc, xp, True, True))
-                q = ("svsv", "sssv")[i][b]
-                done[q] = evacuate(q, T.ht[:, lo + b:lo + 4 * n:4], bank(b0 + b, n), True, m, done[q])
-            q_h.append(op("v", lambda: V.quantize_mx(T.hq[:, HALF * k:HALF * k + n], T.hp[:, HALF * k:HALF * k + n],
-                                                     T.ht[:, lo:lo + 4 * n]), [done["s"]], on=done["v"]))
-        b0 = 4 * (s % 2)
-        lo = 4 * HALF * s
-        wait("t", l_c)
+    def take(b0):
+        for e in free[b0]:
+            wait("t", e)
+
+    q_h = {}
+
+    def layer_a(s, i, b0, xc, xp, n, skip, by):
+        take(b0)
+        k = 2 * s + i
+        lo = 4 * FAR * k
         done = {"s": None, "v": None}
-        for i in range(2):
-            k = 2 * s + i
-            wait("t", q_h[i])
-            for b in range(4):
-                w = 512 * i + 128 * b
-                call = lambda: PE.matmul_mx(bank(b0 + b, n), T.cq[:, w:w + 128], T.cpl[:, w:w + 128],
-                                            T.hq[:, HALF * k:HALF * k + n], T.hp[:, HALF * k:HALF * k + n], i == 0, i == 1)
-                if i == 0:
-                    call()
-                else:
-                    m = op("t", call)
-                    q = "svsv"[b]
-                    done[q] = evacuate(q, T.zt[:, lo + b:lo + 4 * n:4], bank(b0 + b, n), False, m, done[q])
-        q_z.append(op("v", lambda: V.quantize_mx(oq, osc, T.zt[:, lo:lo + 4 * n]), [done["s"]], on=done["v"]))
+        for b in range(4):
+            w = 512 * i + 128 * b
+            m = op("t", lambda: PE.matmul_mx(bank(b0 + b, n), T.aq[:, w:w + 128], T.apl[:, w:w + 128], xc, xp, True, True))
+            done[by[b]] = evacuate(by[b], T.ht[:, lo + 4 * skip + b:lo + 4 * n:4], bank(b0 + b, n - skip, skip), True, m, done[by[b]])
+        free[b0] = [list(e) for e in done.values() if e]
+        q_h[k] = op("v", lambda: V.quantize_mx(T.hq[:, FAR * k:FAR * k + n], T.hp[:, FAR * k:FAR * k + n], T.ht[:, lo:lo + 4 * n]),
+                    [done["s"], pad], on=done["v"])
+        return m
+
+    def layer_c(s, i, b0, n, skip=0, oq=None, osc=None, by="svsv"):
+        k = 2 * s + i
+        lo = 4 * FAR * s
+        if i == 0:
+            take(b0)
+        wait("t", l_c)
+        wait("t", q_h[k])
+        done = {"s": None, "v": None}
+        for b in range(4):
+            w = 512 * i + 128 * b
+            call = lambda: PE.matmul_mx(bank(b0 + b, n), T.cq[:, w:w + 128], T.cpl[:, w:w + 128],
+                                        T.hq[:, FAR * k:FAR * k + n], T.hp[:, FAR * k:FAR * k + n], i == 0, i == 1)
+            if i == 0:
+                call()
+            else:
+                m = op("t", call)
+                done[by[b]] = evacuate(by[b], T.zt[:, lo + 4 * skip + b:lo + 4 * n:4], bank(b0 + b, n - skip, skip), False, m, done[by[b]])
+        if i == 1:
+            free[b0] = [list(e) for e in done.values() if e]
+            return op("v", lambda: V.quantize_mx(oq, osc, T.zt[:, lo:lo + 4 * n]), [done["s"]], on=done["v"])
 
     def home(b0, zc, zp, n, at, m_cols, col, whole):
         out = []
+        take(b0)
         for b in range(4):
             m = op("t", lambda: PE.matmul_mx(bank(b0 + b, n), T.eq[:, 128 * b:128 * b + 128], T.ep[:, 128 * b:128 * b + 128], zc, zp, True, True))
             out.append(op("v", lambda: V.tensor_tensor(T.hw[:, HW * b + col:HW * b + col + m_cols], bank(b0 + b, m_cols, at),
                                                        T.xt[:, 4 * col + b:4 * (col + m_cols):4], A.add), [m], join=out[0] if whole and out else None))
+        free[b0] = [out[-1]]
         return out
 
-    a0 = 0 if me["first"] else HALF - 128
-    wait("t", l_a)
-    wait("t", q_b[1])
-    expert(0, T.x2q[:, a0:a0 + 128], T.x2p[:, a0:a0 + 128], 128, T.z0q[:], T.z0p[:])
-    q_e = op("v", lambda: V.quantize_mx(T.eq[:], T.ep[:], T.et[:]), [e_t])
-    PE.wait_ge(T.sem.xfar, far_count)
-    expert(1, T.x1lq[:], T.x1lp[:], HALF, T.z1q[:], T.z1p[:])
-    send_far("z", q_z[1])
-    PE.wait_ge(T.sem.xnear, near_count)
-    expert(2, T.x2lq[:], T.x2lp[:], 3 * C, T.z2q[:], T.z2p[:])
-    send_near("z", q_z[2])
-
-    h_x = None
-    for t in range(4):
-        h_x = op("s", lambda: S.activation(T.hw[:, HW * t + N * C:HW * (t + 1)], T.xpl[:, TC * t:TC * (t + 1)], ACT.Copy), [pl], join=h_x)
-    wait("t", q_e)
-    wait("t", q_z[0])
-    s_own = home(4, T.z0q[:], T.z0p[:], 128, own - HALF - a0, C, own, True)[0]
     n14 = slice(0, 14)
-    e = op("v", lambda: V.tensor_scalar(T.d0[:, n14], T.r9[:, 7:112:8], -BIG, None, A.add), [e_r9])
-    op("v", lambda: V.tensor_scalar(T.dd[:], T.pidx[:, 0:2], 15, None, A.bitwise_and), join=e)
-    e = op("v", lambda: V.tensor_scalar(T.d1[:, n14], T.d0[:, n14], 9, None, A.logical_shift_right), [e])
-    op("v", lambda: V.tensor_scalar(T.d2[:, n14], T.d0[:, n14], STRIDE - 1, None, A.bitwise_and), join=e)
-    op("v", lambda: V.tensor_copy(T.de[:], T.dd[:]), join=e)
-    e = op("v", lambda: V.tensor_scalar(T.d3[:, n14], T.d1[:, n14], 2.0 * C, float(C - STRIDE // 2), A.mult, A.add), [e])
-    op("v", lambda: V.tensor_scalar(T.d4[:, n14], T.d2[:, n14], 0.5 - STRIDE // 2, None, A.add), join=e)
-    op("v", lambda: V.tensor_scalar(T.d5[:, n14], T.dc[:, n14], T.de[:, 0:1], None, A.add), [c_d], join=e)
-    e = op("v", lambda: V.tensor_tensor(T.d6[:, n14], T.d3[:, n14], T.d2[:, n14], A.add), [e])
-    op("v", lambda: V.tensor_tensor(T.d7[:, n14], T.d4[:, n14], T.d4[:, n14], A.mult), join=e)
-    e = op("v", lambda: V.tensor_tensor(T.d8[:, n14], T.d6[:, n14], T.d5[:, n14], A.subtract), [e])
-    op("v", lambda: V.tensor_scalar(T.d9[:, n14], T.d7[:, n14], float(C * C), None, A.is_lt), join=e)
-    e = op("v", lambda: V.tensor_tensor(T.da[:, n14], T.d8[:, n14], T.d9[:, n14], A.mult), on=e)
-    e = op("v", lambda: V.tensor_tensor(T.db[:, n14], T.da[:, n14], T.d5[:, n14], A.add), on=e)
-    e_hl = op("v", lambda: V.tensor_copy(T.hl[:, n14], T.db[:, n14]), on=e)
+    own = (T.x2q[:, FAR - 128:FAR], T.x2p[:, FAR - 128:FAR], 128, PAD)
+    wait("t", l_a)
+    wait("t", q_own)
+    e = op("v", lambda: V.tensor_copy(T.d0[:, n14], T.sl[:, n14]))
+    op("v", lambda: V.tensor_scalar(T.d5[:, n14], T.dc[:, n14], T.pcT[:, 96:97], None, A.add), [c_d], join=e)
+    e = op("v", lambda: V.tensor_scalar(T.d1[:, n14], T.d0[:, n14], 8, 7, A.logical_shift_right, A.bitwise_and), on=e)
+    op("v", lambda: V.tensor_scalar(T.d2[:, n14], T.d0[:, n14], RUN - 1, None, A.bitwise_and), join=e)
+    layer_a(0, 0, 0, *own, BY[0])
+    e = op("v", lambda: V.tensor_scalar(T.d3[:, n14], T.d1[:, n14], float(C), -16.0, A.mult, A.add), on=e)
+    op("v", lambda: V.tensor_scalar(T.d4[:, n14], T.d2[:, n14], 16.0 + C, 1024.0, A.is_ge, A.mult), join=e)
+    layer_a(0, 1, 4, *own, BY[1])
+    e = op("v", lambda: V.tensor_tensor(T.d6[:, n14], T.d3[:, n14], T.d2[:, n14], A.add), on=e)
+    e = op("v", lambda: V.tensor_tensor(T.d7[:, n14], T.d6[:, n14], T.d4[:, n14], A.add), on=e)
+    e = op("v", lambda: V.tensor_tensor(T.d8[:, n14], T.d7[:, n14], T.d5[:, n14], A.min), on=e)
+    layer_c(0, 0, 0, 128)
+    q_z0 = layer_c(0, 1, 0, 128, PAD, T.z0q[:], T.z0p[:], BY[2])
+    e_hl = op("v", lambda: V.tensor_copy(T.hl[:, n14], T.d8[:, n14]), on=e)
+
+    far, near = (T.x1lq[:], T.x1lp[:], FAR, 0), (T.x2lq[:], T.x2lp[:], NEAR, 0)
+    PE.wait_ge(T.sem.xfar, far_count)
+    m = layer_a(1, 0, 4, *far, BY[3])
+    l_v = op("q", lambda: Q.dma_start(T.vs[:], T.v[:]), [m], inc=16)
+    layer_a(1, 1, 0, *far, BY[4])
+    PE.wait_ge(T.sem.xnear, near_count)
+    layer_a(2, 0, 4, *near, BY[5])
+    layer_c(1, 0, 0, FAR)
+    send_far("z", layer_c(1, 1, 0, FAR, 0, T.z1q[:], T.z1p[:], BY[6]))
+    layer_a(2, 1, 4, *near, BY[7])
+    layer_c(2, 0, 0, NEAR)
+    send_near("z", layer_c(2, 1, 0, NEAR, 0, T.z2q[:], T.z2p[:], BY[8]))
+    q_e = None
+    for b in range(4):
+        q_e = op("v", lambda: V.quantize_mx(T.eq[:, 128 * b:128 * b + 128], T.ep[:, 128 * b:128 * b + 128], T.eb[:, 3 - b:515 - b]), [c_e], join=q_e)
+
+    wait("t", q_e)
+    wait("t", q_z0)
+    s_own = home(4, T.z0q[:], T.z0p[:], 128, 128 - C, C, 7 * C, True)[0]
     q_v = op("v", lambda: V.quantize_mx(T.vq[:], T.vp[:], T.vs[:]), [l_v])
     e = op("s", lambda: S.activation(T.olb[:], T.tab[:, 0:HW].indirect(T.hl[:, n14]), ACT.Copy), [e_hl, c_tab])
     stores = op("q", lambda: Q.dma_start(T.ol[:], T.olb[0:128:16, :]), [e], inc=16)
 
-    wait("t", q_z[2])
     PE.wait_ge(T.sem.zfar, far_count)
-    s_far = home(0, T.z1lq[:], T.z1lp[:], HALF, 0, HALF, 0, True)[0]
-    wait("t", s_own)
+    s_first = home(0, T.z1lq[:], T.z1lp[:], FAR, 0, FAR, 0, True)[0]
     PE.wait_ge(T.sem.znear, near_count)
-    s_near = home(4, T.z2lq[:], T.z2lp[:], 3 * C, 0, 3 * C, near0, False)
+    s_last = home(4, T.z2lq[:], T.z2lp[:], NEAR, 0, NEAR, FAR, False)
     gs = None
     for b, k in ((0, 14), (1, 14), (2, 8)):
         gs = op("s", lambda: S.activation(T.yt[:, b:64 * k:4], T.hw[:, HW * b:HW * (b + 1)].indirect(T.hl[:, 0:k]), ACT.Copy),
-                [h_x, s_own, s_far, s_near[b]], join=gs)
-    gv = op("v", lambda: V.tensor_copy(T.yt[:, 512 + 2:4 * TC:4], T.hw[:, HW * 2:HW * 3].indirect(T.hl[:, 8:14])), [h_x, s_own, s_far, e_hl, s_near[2]])
-    op("v", lambda: V.tensor_copy(T.yt[:, 3:4 * TC:4], T.hw[:, HW * 3:HW * 4].indirect(T.hl[:, n14])), [s_near[3]], join=gv)
+                [h_x, s_own, s_first, s_last[b]], join=gs)
+    gv = op("v", lambda: V.tensor_copy(T.yt[:, 512 + 2:4 * TC:4], T.hw[:, HW * 2:HW * 3].indirect(T.hl[:, 8:14])), [h_x, s_own, s_first, e_hl, s_last[2]])
+    op("v", lambda: V.tensor_copy(T.yt[:, 3:4 * TC:4], T.hw[:, HW * 3:HW * 4].indirect(T.hl[:, n14])), [s_last[3]], join=gv)
     q_y = op("v", lambda: V.quantize_mx(T.yq[:], T.yp[:], T.yt[:]), [gs], on=gv)
+    take(0)
     m = op("t", lambda: PE.matmul_mx(bank(0, TC), T.vq[:], T.vp[:], T.yq[:], T.yp[:], True, True), [q_v, q_y])
     op("q", lambda: Q.dma_start(T.oc[:], _u8(T.yq[:])), [q_y], join=stores, inc=16)
     for k in range(4):

@@ -2,13 +2,16 @@ from concourse.bass import DstId, RemoteDMATransfer
 from concourse.mybir import dt, AluOpType, ActivationFunctionType
 
 N, TC, C = 8, 224, 48
-FAR, NEAR = 4 * C, 3 * C
+FAR, NEAR, ALL = 4 * C, 3 * C, 7 * C
 PAD = 128 - C
 SEG = TC // 2
-RUN, LANE = 256, 2048
+LANE = 256
 HW = 8 * C + TC
 F8, U8, U16, BF, F32, I32 = "float8_e4m3fn_x4", "uint8", "uint16", "bfloat16", "float32", "int32"
-BY = ["svsv", "sssv", "svsv", "svsv", "sssv", "sssv", "svsv", "sssv", "svsv"]
+BIG = 1e29
+ORDER = "2a0:4 2a1:0 1a0:4 1a1:0 1c0:4 1c1:4 2c0:0 2c1:0"
+BY = "svsv sssv svsv svsv sssv svsv sssv svsv svsv"
+HOME = "21"
 
 
 def _sb(n, d):
@@ -22,22 +25,22 @@ SCRATCH = {
     "uq2": _sb(128, F8), "up2": _sb(128, U8), "vq": _sb(128, F8), "vp": _sb(128, U8),
     "aq": _sb(1024, F8), "apl": _sb(1024, U8), "cq": _sb(1024, F8), "cpl": _sb(1024, U8),
     "pidx": _sb(8, I32), "i16": _sb(8, I32), "t0": _sb(8, I32), "t1": _sb(8, I32), "uoff": _sb(8, U16),
-    "pc": _sb(128, F32), "pcT": _sb(128, F32), "mlist": _sb(8, U16), "glist": _sb(2, U16),
-    "jv": _sb(TC, BF), "pmax": _sb(SEG, F32), "crow": _sb(TC, BF), "im": _sb(C, BF), "diag": _sb(C, BF),
-    "pt": _sb(TC, F32), "rm": _sb(152, F32), "rn": _sb(SEG, F32), "ee": _sb(SEG + 8, BF), "gs": _sb(TC, BF), "gT": _sb(TC, BF),
-    "val": _sb(TC, F32), "vT": _sb(TC, F32), "tw": _sb(32 + 512, F32), "tu": _sb(64, F32), "sl": _sb(16, U16),
+    "pc": _sb(64, F32), "pcT": _sb(64, F32), "glist": _sb(2, U16), "crT": _sb(TC, BF),
+    "jv": _sb(TC, BF), "pf": _sb(64, F32), "pb": _sb(64, F32), "crow": _sb(TC, BF), "im": _sb(C, BF), "diag": _sb(C, BF),
+    "pt": _sb(TC, F32), "rf": _sb(SEG, F32), "rb": _sb(128, F32), "ee": _sb(SEG + 8, BF), "gs": _sb(TC, BF), "gT": _sb(TC, BF),
+    "val": _sb(TC, BF), "vT": _sb(TC, BF), "mm": _sb(SEG, F32), "tw": _sb(32 + 512, F32), "tu": _sb(64, F32), "sl": _sb(16, U16),
+    "hb": _sb(SEG, F32), "tw2": _sb(32 + 512, F32), "tu2": _sb(64, F32),
     "win": _sb(N * LANE, BF), "ex": _sb(N * C, BF), "il": _sb(32, U16),
-    "xpl": _sb(4 * TC, BF), "xt": _sb(4 * N * C, BF),
-    "x1q": _sb(FAR, F8), "x1p": _sb(FAR, U8), "x1lq": _sb(FAR, F8), "x1lp": _sb(FAR, U8),
-    "x2q": _sb(FAR, F8), "x2p": _sb(FAR, U8), "x2lq": _sb(NEAR, F8), "x2lp": _sb(NEAR, U8),
-    "z0q": _sb(128, F8), "z0p": _sb(128, U8),
-    "z1q": _sb(FAR, F8), "z1p": _sb(FAR, U8), "z1lq": _sb(FAR, F8), "z1lp": _sb(FAR, U8),
-    "z2q": _sb(NEAR, F8), "z2p": _sb(NEAR, U8), "z2lq": _sb(NEAR, F8), "z2lp": _sb(NEAR, U8),
+    "xpl": _sb(4 * TC, BF), "xt": _sb(4 * (PAD + N * C), BF),
+    "x0q": _sb(128, F8), "x0p": _sb(128, U8), "x1q": _sb(FAR, F8), "x1p": _sb(FAR, U8), "x2q": _sb(NEAR, F8), "x2p": _sb(NEAR, U8),
+    "xlq": _sb(ALL, F8), "xlp": _sb(ALL, U8),
+    "z0q": _sb(128, F8), "z0p": _sb(128, U8), "z1q": _sb(FAR, F8), "z1p": _sb(FAR, U8), "z2q": _sb(NEAR, F8), "z2p": _sb(NEAR, U8),
+    "zlq": _sb(ALL, F8), "zlp": _sb(ALL, U8),
     "rxq": _sb(2 * C, F8), "rxp": _sb(2 * C, U8), "rzq": _sb(2 * C, F8), "rzp": _sb(2 * C, U8),
     "ht": _sb(24 * FAR, BF), "hq": _sb(6 * FAR, F8), "hp": _sb(6 * FAR, U8), "zt": _sb(12 * FAR, BF),
     "eb": _sb(516, BF), "eq": _sb(512, F8), "ep": _sb(512, U8),
     "hw": _sb(4 * HW, BF), "tab": _sb(HW, F32), "olb": _sb(TC, F32),
-    "d0": _sb(16, I32), "d1": _sb(16, I32), "d2": _sb(16, I32), "d3": _sb(16, F32), "d4": _sb(16, F32),
+    "d0": _sb(16, I32), "d1": _sb(16, I32), "d2": _sb(16, I32), "d3": _sb(16, I32), "d4": _sb(16, F32),
     "d5": _sb(16, F32), "d6": _sb(16, F32), "d7": _sb(16, F32), "d8": _sb(16, F32), "dc": _sb(16, F32), "hl": _sb(16, U16),
     "yt": _sb(4 * TC, BF), "yq": _sb(TC, F8), "yp": _sb(TC, U8), "yo": _sb(TC, F32),
 }
@@ -56,23 +59,28 @@ def _plan(T, topo):
     plan = []
     for r in range(N):
         far = [d for d in range(N) if d != r and not topo.may_write(cores[r], cores[d])]
-        near = [d for d in range(N) if d not in far and d != r]
+        mine = [d for d in range(N) if d not in far]
         assert len(far) == 4
-        far = far[r // 2:] + far[:r // 2]
+        i = mine.index(r)
+        far = far[i:] + far[:i]
+        near = [mine[i ^ k] for k in (1, 2, 3)]
         able = [c for c in topo.cores_of(cores[r]) if c not in cores and all(topo.may_write(c, cores[d]) for d in far)]
         same = [c for c in able if topo.die(c) == topo.die(cores[r])]
         across = [c for c in able if topo.die(c) != topo.die(cores[r])]
-        plan.append({"order": far + near + [r], "codes": [same[0], across[0]], "scales": [same[1], across[1]], "near": near})
+        plan.append({"order": far + near + [r], "codes": [across[0], same[0]], "scales": [across[1], same[1]]})
     return plan
 
 
-def _near_masks(topo, src, dst):
+def _near_masks(topo, src, dst, stage):
     e = topo.engines(src, dst)
-    h, q = len(e) // 2, len(e) // 4
-    return [e[:h], e[h:h + q], e[h + q:]], [e[:q], e[q:h], e[h:]]
+    a, b = e[0::2], e[1::2]
+    q = len(a) // 2
+    if stage == "x":
+        return [e, a, b], [e, a, b]
+    return [a, b[:q], b[q:]], [a[:q], a[q:], b]
 
 
-def _hand_engines(topo, plan, T, r, stage, kind, t):
+def _hand_engines(topo, plan, T, r, kind, t):
     return topo.engines(T.cores[r], plan[r][kind][t])[t::2]
 
 
@@ -92,7 +100,7 @@ def _helper(g, core, T, topo, plan):
                 t = plan[r][kind].index(core)
                 total = 0
                 for stage in ("x", "z"):
-                    g.wait_ge(T.sem["r" + stage], len(_hand_engines(topo, plan, T, r, stage, kind, t)))
+                    g.wait_ge(T.sem["r" + stage], len(_hand_engines(topo, plan, T, r, kind, t)))
                     tr = []
                     for k in range(2):
                         d = plan[r]["order"][2 * t + k]
@@ -100,9 +108,9 @@ def _helper(g, core, T, topo, plan):
                         e = e[k * (len(e) // 2):(k + 1) * (len(e) // 2)]
                         at = C * plan[d]["order"].index(r)
                         if kind == "codes":
-                            src, dst = _u8(T["r%sq" % stage][:, C * k:C * k + C]), _u8(T[stage + "1lq"][:, at:at + C])
+                            src, dst = _u8(T["r%sq" % stage][:, C * k:C * k + C]), _u8(T[stage + "lq"][:, at:at + C])
                         else:
-                            src, dst = T["r%sp" % stage][:, C * k:C * k + C], T[stage + "1lp"][:, at:at + C]
+                            src, dst = T["r%sp" % stage][:, C * k:C * k + C], T[stage + "lp"][:, at:at + C]
                         tr.append(RemoteDMATransfer(dst_ids=[_dst(topo, T.cores[d], core)], dma_engine_mask=_mask(e),
                                                     remote_sem=T.sem[stage + "far"], src=src, dst=dst))
                         total += len(e)
@@ -122,6 +130,7 @@ def rank_program(g, core, T, topo):
     queues = {"g": g, "v": V, "s": S, "t": PE, "q": Q}
     A, ACT = AluOpType, ActivationFunctionType
     top, seen, used = {}, {}, [0]
+    by_stage = BY.split()
 
     def wait(q, e):
         if seen.get((q, e[0]), 0) < e[1]:
@@ -130,7 +139,8 @@ def rank_program(g, core, T, topo):
 
     def op(q, call, deps=(), join=None, on=None, inc=1):
         for e in deps:
-            wait(q, e)
+            if e:
+                wait(q, e)
         if on is not None:
             wait(q, on)
             assert top[on[0]] == on[1]
@@ -157,7 +167,11 @@ def rank_program(g, core, T, topo):
         return op("v", lambda: V.memset(view, value), join=join)
 
     def run(d):
-        return LANE * (N - 1 - d) + RUN * order.index(d) + 16
+        return LANE * (N - 1 - d) + 16
+
+    def xt(c0, c1, b=None):
+        lo, hi = (4 * c0, 4 * c1) if c0 < FAR else (4 * (PAD + c0), 4 * (PAD + c1))
+        return T.xt[:, lo:hi] if b is None else T.xt[:, lo + b:hi:4]
 
     l_u = op("q", lambda: Q.dma_start(T.us[:], T.u[:]), inc=16)
     l_xa = op("q", lambda: Q.dma_start(T.xs[:, 0:512], T.x[:, 0:512]), inc=16)
@@ -169,95 +183,111 @@ def rank_program(g, core, T, topo):
 
     c_p = iota(T.pidx[:], [[0, 8]], 0, 1)
     iota(T.i16[:], [[16, 8]], 0, join=c_p)
-    c_pc = None
+    c_pc = iota(T.pc[:, 0:32], [[0, 2], [1, 16]], 0)
     for h in range(2):
         for par in range(2):
-            view = T.pc[:, 64 + 16 * h + par:80 + 16 * h:2]
-            c_pc = iota(view, [[16, 8]], 32 + 8 * h + 7, join=c_pc) if par == h else iota(view, [[1, 8]], 0, join=c_pc)
-    iota(T.pc[:, 96:128], [[0, 2], [1, 16]], 0, join=c_pc)
+            view = T.pc[:, 32 + 16 * h + par:48 + 16 * h:2]
+            iota(view, [[16, 8]], 32 + 8 * h + 7, join=c_pc) if par == h else iota(view, [[1, 8]], 0, join=c_pc)
     c_j = iota(T.jv[:], [[1, TC]], 0)
     iota(T.im[:], [[0, 3], [1, 16]], 0, join=c_j)
-    c_d = iota(T.dc[:], [[16, 16]], N * C)
     c_w = None
     for d in order:
         c_w = iota(T.win[:, run(d):run(d) + C], [[0, C]], TC - 1, join=c_w)
-    c_e = iota(T.eb[:], [[0, 516]], 1)
-    c_e = op("g", lambda: g.affine_select(T.eb[:], T.eb[:], [[1, 516]], A.is_equal, 0.0, -3, -4), on=c_e)
 
-    m0 = fill(T.pmax[:], 0.0)
-    m_pc = fill(T.pc[:, 7:32:8], 64.0)
-    for k in range(4):
-        fill(T.pc[:, 8 * k:8 * k + 7], 8.0 * (k % 2) + 7.0, m_pc)
-    for d in range(N):
-        fill(T.pc[:, 32 + 2 * d:64:16], run(d) - 1.0, m_pc)
-    fill(T.pc[:, 33:64:2], 0.0, m_pc)
+    m0 = fill(T.pf[:], 0.0)
+    fill(T.pb[:], 0.0, m0)
+    fill(T.crT[:], 0.0, m0)
+    c_e = fill(T.eb[:], 1.0)
+    m2 = op("v", lambda: V.memset(T.crT[:, 2 * (N - 1):TC:16], 1.0), [m0])
     e = op("v", lambda: V.tensor_scalar(T.t0[:], T.pidx[:], 1, 7, A.logical_shift_right, A.bitwise_and), [c_p])
-    m1 = fill(T.rm[:, 64:72], 1e29)
-    fill(T.rm[:, 128:152], 1e29, m1)
+    m1 = fill(T.rb[:, 64:128:56], BIG)
     fill(T.ee[:, 0:1], 0.0, m1)
     e = op("v", lambda: V.tensor_tensor(T.t1[:], T.t0[:], T.i16[:], A.add), on=e)
     fill(T.gs[:, 1:TC:2], 0.0, m1)
     fill(T.tw[:, 32 + SEG + 7:544:8], 0.0, m1)
     c_uo = op("v", lambda: V.tensor_copy(T.uoff[:], T.t1[:]), on=e)
-    op("v", lambda: V.memset(T.pmax[:, 0:SEG:8], -1e29), [m0], join=m1)
-    c_t = op("v", lambda: V.transpose(T.pcT[:], T.pc[:]), [c_pc, m_pc])
+    fill(T.pf[:, 0:64:8], -BIG, m1)
+    fill(T.pb[:, 0:64:8], -9 * BIG, m1)
+    fill(T.pb[:, 7:64:8], BIG, m1)
+    op("v", lambda: V.transpose(T.crow[:], T.crT[:]), [m2], join=m1)
+    c_e = op("g", lambda: g.affine_select(T.eb[:], T.eb[:], [[1, 516]], A.is_equal, 0.0, -3, -4), [c_e])
 
     q_u = op("v", lambda: V.quantize_mx(T.uq[:], T.up[:], T.us[:]), [l_u])
-    c_l = op("v", lambda: V.tensor_scalar(T.mlist[:], T.i16[:], T.pcT[:, 0:1], 64.0, A.add, A.min), [c_t])
+    f2 = fill(T.tw2[:, 32 + SEG + 7:544:8], 0.0)
     k_u = op("v", lambda: V.tensor_copy(T.uq2[:, 0:128].bitcast(dt.uint32), T.uq[:, 0:128].bitcast(dt.uint32).indirect(T.uoff[:, 0:8])), [q_u, c_uo])
     k_s = op("s", lambda: S.activation(T.up2[:, 0:128], T.up[:, 0:128].indirect(T.uoff[:, 0:8]), ACT.Copy), [q_u, c_uo])
     q_xa = op("v", lambda: V.quantize_mx(T.xq[:, 0:128], T.xp[:, 0:128], T.xs[:, 0:512]), [l_xa])
     m_a = op("t", lambda: PE.matmul_mx(bank(0, 128), T.uq2[:], T.up2[:], T.xq[:, 0:128], T.xp[:, 0:128], True, True), [k_u, k_s, q_xa])
-    op("v", lambda: V.tensor_scalar(T.crow[:], T.jv[:], run(N - 1) - 1.0, T.pcT[:, 32:33], A.add, A.is_ge), [c_j], join=c_l)
     q_xb = op("v", lambda: V.quantize_mx(T.xq[:, 128:256], T.xp[:, 128:256], T.xs[:, 4 * TC - 512:4 * TC]), [l_xb])
     m_b = op("t", lambda: PE.matmul_mx(bank(1, 128), T.uq2[:], T.up2[:], T.xq[:, 128:256], T.xp[:, 128:256], True, True), [q_xb])
     pl = None
     for t in range(4):
         pl = op("s", lambda: S.activation(T.xpl[:, TC * t:TC * t + TC], T.xs[:, t:4 * TC:4], ACT.Copy), [l_xa, l_xb], join=pl)
-    h_x = None
-    for t in range(4):
-        h_x = op("s", lambda: S.activation(T.hw[:, HW * t + N * C:HW * (t + 1)], T.xs[:, t:4 * TC:4], ACT.Copy), join=h_x)
-    pad = None
-    for tile in (T.ht[:, 0:4 * PAD], T.ht[:, 4 * FAR:4 * (FAR + PAD)], T.zt[:, 0:4 * PAD]):
-        pad = op("s", lambda: S.activation(tile, T.xs[:, 0:4 * PAD], ACT.Identity, scale=0.0), join=pad)
 
-    cols, segs, wins = ((0, 128), (128, TC)), ((0, 64), (64, SEG)), (0, 80)
+    cols, segs, wins = ((0, 128), (128, TC)), ((0, 64), (64, SEG)), (0, 72)
+    lanes = {}
+
+    def back(buf, lo, hi, st):
+        last = lo + (hi - lo - 1) // st * st
+        return buf[:, last::-st] if lo < st else buf[:, last:lo - st:-st]
 
     def step(k, h, deps=(), on=None):
         (c0, c1), (s0, s1), w = cols[h], segs[h], wins[h]
+        n = s1 - s0
         if k == 0:
             return op("v", lambda: V.transpose(T.pt[:, c0:c1], bank(h, c1 - c0, 128 - (c1 - c0))), deps, on=on)
         if k == 1:
-            e = op("v", lambda: V.tensor_tensor_scan(T.rm[:, w:w + s1 - s0], T.pmax[:, s0:s1], T.pt[:, c0:c1:2], 0.0, A.add, A.max), deps, on=on)
-            return op("v", lambda: V.tensor_tensor_scan(T.rn[:, s0:s1], T.pmax[:, s0:s1], T.pt[:, c0:c1:2], 0.0, A.add, A.max), join=e)
+            e = op("v", lambda: V.tensor_tensor_scan(T.rf[:, s0:s1], T.pf[:, 0:n], T.pt[:, c0:c1:2], 0.0, A.add, A.max), deps, on=on)
+            return op("v", lambda: V.tensor_tensor_scan(back(T.rb, w, w + n, 1), T.pb[:, 0:n], back(T.pt, c0, c1, 2), 0.0, A.add, A.max), join=e)
         if k == 2:
-            return op("v", lambda: V.tensor_tensor(T.ee[:, s0 + 1:s1 + 1], T.rm[:, w:w + 72].indirect(T.mlist[:, 0:(s1 - s0) // 16]), T.rn[:, s0:s1], A.is_equal), deps, on=on)
+            return op("v", lambda: V.tensor_tensor(T.ee[:, s0 + 1:s1 + 1], T.rf[:, s0:s1], T.rb[:, w + 1:w + 1 + n], A.is_ge), deps, on=on)
         if k == 3:
+            lanes[h] = op("s", lambda: S.activation(T.mm[:, s0:s1], T.ee[:, s0:s1], ACT.Identity, scale=4096.0 + LANE, bias=-4096.0), [on])
             return op("v", lambda: V.tensor_tensor(T.gs[:, c0:c1:2], T.ee[:, s0 + 1:s1 + 1], T.ee[:, s0:s1], A.subtract), deps, on=on)
         if k == 4:
             return op("v", lambda: V.transpose(T.gT[:, c0:c1], T.gs[:, c0:c1]), deps, on=on)
         if k == 5:
-            first = T.val[:, c0 - 1:c0] if h else T.pcT[:, 32:33]
+            first = T.val[:, c0 - 1:c0] if h else 15.0
             return op("v", lambda: V.tensor_tensor_scan(T.val[:, c0:c1], T.crow[:, c0:c1], T.gT[:, c0:c1], first, A.add, A.add), deps, on=on)
         if k == 6:
             return op("v", lambda: V.transpose(T.vT[:, c0:c1], T.val[:, c0:c1]), deps, on=on)
-        return op("v", lambda: V.tensor_tensor_scan(T.tw[:, 32 + s0:32 + s1], T.ee[:, s0:s1], T.vT[:, c0:c1:2], 0.0, A.mult, A.max), deps, on=on)
+        return op("v", lambda: V.tensor_tensor_scan(T.tw[:, 32 + s0:32 + s1], T.mm[:, s0:s1], T.vT[:, c0:c1:2], 0.0, A.add, A.max), [lanes[h]], on=on)
+
+    def swap(tw, tu, out, e, deps=()):
+        e = op("v", lambda: V.transpose(tu[:, 0:32], tw[:, 39:544:16]), on=e)
+        op("v", lambda: V.transpose(tu[:, 32:64], tw[:, 47:544:16]), join=e)
+        yield None
+        e = op("v", lambda: V.transpose(tw[:, 0:32], tu[:, 16:48]), on=e)
+        yield None
+        yield op("v", lambda: V.tensor_scalar(out, tw[:, 0:32 + SEG].indirect(T.glist[:, 0:1]), 0.0, None, A.add), deps, on=e)
 
     ea = step(0, 0, [m_a, m1])
-    op("v", lambda: V.tensor_scalar(T.glist[:], T.pcT[:, 64:66], 31.0 + SEG, None, A.min), join=c_l)
-    op("v", lambda: V.tensor_scalar(T.diag[:], T.im[:], T.pcT[:, 96:97], 512.0, A.is_equal, A.mult), join=c_l)
     ea = step(1, 0, on=ea)
     eb = step(0, 1, [m_b])
     for k in range(2, 8):
-        ea = step(k, 0, [c_l], on=ea)
+        ea = step(k, 0, on=ea)
         eb = step(k - 1, 1, on=eb)
+        if k == 4:
+            c_t = op("v", lambda: V.transpose(T.pcT[:], T.pc[:]), [c_pc])
+        if k == 6:
+            c_l = op("v", lambda: V.tensor_scalar(T.glist[:], T.pcT[:, 32:34], 31.0 + SEG, None, A.min), [c_t])
+        if k == 7:
+            op("v", lambda: V.tensor_scalar(T.diag[:], T.im[:], T.pcT[:, 0:1], 512.0, A.is_equal, A.mult), [c_j], join=c_l)
     e = step(7, 1, on=eb)
     wait("v", ea)
-    e = op("v", lambda: V.transpose(T.tu[:, 0:32], T.tw[:, 39:544:16]), on=e)
-    op("v", lambda: V.transpose(T.tu[:, 32:64], T.tw[:, 47:544:16]), join=e)
-    e = op("v", lambda: V.transpose(T.tw[:, 0:32], T.tu[:, 16:48]), on=e)
-    e_sl = op("v", lambda: V.tensor_scalar(T.sl[:], T.tw[:, 0:32 + SEG].indirect(T.glist[:, 0:1]), 0.0, None, A.add), on=e)
+    e_sl = list(swap(T.tw, T.tu, T.sl[:], e, [c_l]))[-1]
     e_sc = op("v", lambda: V.tensor_copy(T.win[:, 0:N * LANE].indirect(T.sl[:, 0:14]), T.jv[:]), [c_w, e_sl])
+
+    copied = (2, 3)
+    pad = None
+    for tile in (T.xt[:, 4 * FAR:4 * (FAR + PAD)], T.ht[:, 0:4 * PAD], T.ht[:, 4 * FAR:4 * (FAR + PAD)], T.zt[:, 0:4 * PAD]):
+        pad = op("s", lambda: S.activation(tile, T.xs[:, 0:4 * PAD], ACT.Identity, scale=0.0), join=pad)
+    h_x = None
+    for t in range(4):
+        if t in copied:
+            h_x = op("s", lambda: S.activation(T.hw[:, HW * t + N * C:HW * (t + 1)], T.xs[:, 0:TC], ACT.Identity, scale=0.0), join=h_x)
+        else:
+            h_x = op("s", lambda: S.activation(T.hw[:, HW * t + N * C:HW * (t + 1)], T.xs[:, t:4 * TC:4], ACT.Copy), join=h_x)
 
     sent = [0]
 
@@ -266,68 +296,82 @@ def rank_program(g, core, T, topo):
         for kind in ("codes", "scales"):
             tr = []
             for t in range(2):
-                c = me[kind][t]
-                eng = _hand_engines(topo, plan, T, r, stage, kind, t)
+                eng = _hand_engines(topo, plan, T, r, kind, t)
                 if kind == "codes":
                     src, dst = _u8(T[stage + "1q"][:, 2 * C * t:2 * C * (t + 1)]), _u8(T["r%sq" % stage][:])
                 else:
                     src, dst = T[stage + "1p"][:, 2 * C * t:2 * C * (t + 1)], T["r%sp" % stage][:]
-                tr.append(RemoteDMATransfer(dst_ids=[_dst(topo, c, core)], dma_engine_mask=_mask(eng), remote_sem=T.sem["r" + stage], src=src, dst=dst))
+                tr.append(RemoteDMATransfer(dst_ids=[_dst(topo, me[kind][t], core)], dma_engine_mask=_mask(eng), remote_sem=T.sem["r" + stage], src=src, dst=dst))
                 sent[0] += len(eng)
             g.remote_dma_fused(tr, local_sem=T.sem.sent)
 
-    def send_near(stage, dep):
-        wait("g", dep)
-        for kind in range(2):
+    def send_near(stage, dep, ks=(0, 1, 2), kinds=(0, 1), buf="2", at=0):
+        if dep:
+            wait("g", dep)
+        for kind in kinds:
             tr = []
-            for k, d in enumerate(me["near"]):
-                eng = _near_masks(topo, core, T.cores[d])[kind][k]
-                a = C * k
-                b = C * plan[d]["near"].index(r)
+            for k in ks:
+                d = order[4 + k]
+                eng = _near_masks(topo, core, T.cores[d], stage)[kind][k]
+                a = at + C * (k - ks[0])
+                b = C * plan[d]["order"].index(r)
                 if kind == 0:
-                    src, dst = _u8(T[stage + "2q"][:, a:a + C]), _u8(T[stage + "2lq"][:, b:b + C])
+                    src, dst = _u8(T[stage + buf + "q"][:, a:a + C]), _u8(T[stage + "lq"][:, b:b + C])
                 else:
-                    src, dst = T[stage + "2p"][:, a:a + C], T[stage + "2lp"][:, b:b + C]
+                    src, dst = T[stage + buf + "p"][:, a:a + C], T[stage + "lp"][:, b:b + C]
                 tr.append(RemoteDMATransfer(dst_ids=[_dst(topo, T.cores[d], core)], dma_engine_mask=_mask(eng), remote_sem=T.sem[stage + "near"], src=src, dst=dst))
                 sent[0] += len(eng)
             g.remote_dma_fused(tr, local_sem=T.sem.sent)
 
-    far_count = sum(2 * (len(topo.engines(plan[s]["codes"][0], core)) // 2) for s in order[:4])
-    near_count = 0
-    for s in me["near"]:
-        mk = _near_masks(topo, T.cores[s], core)
-        near_count += len(mk[0][plan[s]["near"].index(r)]) + len(mk[1][plan[s]["near"].index(r)])
+    arriving = {"far": sum(2 * (len(topo.engines(plan[s]["codes"][0], core)) // 2) for s in order[:4])}
+    for stage in ("x", "z"):
+        arriving[stage] = sum(len(_near_masks(topo, T.cores[s], core, stage)[kind][plan[s]["order"].index(r) - 4]) for s in order[4:7] for kind in range(2))
+
+    sets, at_il = [(4, 5), (0, 4), (5, 8), (0, 2), (2, 4)], [0, 4, 16, 4, 10]
 
     def pick(b, join=None):
         w = run(order[b])
         return op("v", lambda: V.tensor_tensor_scan(T.ex[:, C * b:C * b + C], T.diag[:], T.win[:, w:w + C], 0.0, A.add, A.min), [e_sc], join=join)
 
-    def listed(hf, e):
-        return op("v", lambda: V.tensor_copy(T.il[:, 12 * hf:12 * hf + 12], T.ex[:, FAR * hf + 15:FAR * (hf + 1):16]), on=e)
+    def listed(s, e):
+        b0, b1 = sets[s]
+        return op("v", lambda: V.tensor_copy(T.il[:, at_il[s]:at_il[s] + 3 * (b1 - b0)], T.ex[:, C * b0 + 15:C * b1:16]), on=e)
 
-    def gather(q, hf, t, e, join):
-        out, src = T.xt[:, 4 * FAR * hf + t:4 * FAR * (hf + 1):4], T.xpl[:, TC * t:TC * (t + 1)].indirect(T.il[:, 12 * hf:12 * hf + 12])
-        if q == "s":
-            return op("s", lambda: S.activation(out, src, ACT.Copy), [e, pl], join=join)
-        return op("v", lambda: V.tensor_copy(out, src), [e, pl], join=join)
+    def gather(q, s, ts, e, join=None):
+        b0, b1 = sets[s]
+        for t in ts:
+            out, src = xt(C * b0, C * b1, t), T.xpl[:, TC * t:TC * (t + 1)].indirect(T.il[:, at_il[s]:at_il[s] + 3 * (b1 - b0)])
+            if q == "s":
+                join = op("s", lambda: S.activation(out, src, ACT.Copy), [e, pl], join=join)
+            else:
+                join = op("v", lambda: V.tensor_copy(out, src), [e, pl], join=join)
+        return join
 
-    ef = en = None
-    for b in range(4):
-        ef = pick(b, ef)
-    for b in (4, 5):
-        en = pick(b, en)
-    ef = listed(0, ef)
-    for b in (6, 7):
-        en = pick(b, en)
-    gv = gather("v", 0, 1, ef, gather("v", 0, 0, ef, None))
-    gs = gather("s", 0, 3, ef, gather("s", 0, 2, ef, None))
-    en = listed(1, en)
-    send_far("x", op("v", lambda: V.quantize_mx(T.x1q[:], T.x1p[:], T.xt[:, 0:4 * FAR]), [gs], on=gv))
-    gv = gather("v", 1, 1, en, gather("v", 1, 0, en, None))
-    gs = gather("s", 1, 3, en, gather("s", 1, 2, en, None))
-    q_own = op("v", lambda: V.quantize_mx(T.x2q[:], T.x2p[:], T.xt[:, 4 * FAR:8 * FAR]), [gs], on=gv)
-    send_near("x", q_own)
+    e1 = pick(4)
+    ef = pick(1, pick(0))
+    e1 = listed(0, e1)
+    ef = pick(3, pick(2, ef))
+    gv = gather("v", 0, (0,), e1)
+    gs = gather("s", 0, (2, 3), e1)
+    ef = listed(1, ef)
+    gv = gather("v", 0, (1,), e1, gv)
+    en = pick(6, pick(5))
+    send_near("x", op("v", lambda: V.quantize_mx(T.x0q[:], T.x0p[:], T.xt[:, 4 * FAR:4 * (FAR + 128)]), [gs, pad], on=gv), (0,), (0,), "0", PAD)
+    gs = gather("s", 4, (1,), ef, gather("s", 1, (2, 3), ef))
+    gv = gather("v", 1, (0,), ef)
+    en = pick(7, en)
+    gv = gather("v", 3, (1,), ef, gv)
+    en = listed(2, en)
+    send_far("x", op("v", lambda: V.quantize_mx(T.x1q[:], T.x1p[:], xt(0, FAR)), [gs], on=gv))
+    send_near("x", None, (0,), (1,), "0", PAD)
+    gs = gather("s", 2, (2, 3), en)
+    gv = gather("v", 2, (0, 1), en)
+    q_own = op("v", lambda: V.quantize_mx(T.x2q[:], T.x2p[:], xt(FAR + C, N * C)), [gs], on=gv)
+    send_near("x", q_own, (1, 2))
 
+    c_d = iota(T.dc[:], [[16, 16]], N * C + 16)
+    for d in range(N):
+        iota(T.hb[:, d:SEG:8], [[0, SEG // 8]], 512 * (N - 1 - d) + C * order.index(d), join=c_d)
     c_tab = None
     for pos in range(N):
         c_tab = iota(T.tab[:, C * pos:C * pos + C], [[1, C]], C * order[pos], join=c_tab)
@@ -359,10 +403,10 @@ def rank_program(g, core, T, topo):
             done[by[b]] = evacuate(by[b], T.ht[:, lo + 4 * skip + b:lo + 4 * n:4], bank(b0 + b, n - skip, skip), True, m, done[by[b]])
         free[b0] = [list(e) for e in done.values() if e]
         q_h[k] = op("v", lambda: V.quantize_mx(T.hq[:, FAR * k:FAR * k + n], T.hp[:, FAR * k:FAR * k + n], T.ht[:, lo:lo + 4 * n]),
-                    [done["s"], pad], on=done["v"])
+                    [done["s"]], on=done["v"])
         return m
 
-    def layer_c(s, i, b0, n, skip=0, oq=None, osc=None, by="svsv"):
+    def layer_c(s, i, b0, n, skip=0, oq=None, osc=None, by=None):
         k = 2 * s + i
         lo = 4 * FAR * s
         if i == 0:
@@ -383,77 +427,118 @@ def rank_program(g, core, T, topo):
             free[b0] = [list(e) for e in done.values() if e]
             return op("v", lambda: V.quantize_mx(oq, osc, T.zt[:, lo:lo + 4 * n]), [done["s"]], on=done["v"])
 
-    def home(b0, zc, zp, n, at, m_cols, col, whole):
-        out = []
+    def home(b0, zc, zp, n, skip, col):
+        out = {}
         take(b0)
-        for b in range(4):
+        wide = n - skip
+        for b in (2, 0, 3, 1):
             m = op("t", lambda: PE.matmul_mx(bank(b0 + b, n), T.eq[:, 128 * b:128 * b + 128], T.ep[:, 128 * b:128 * b + 128], zc, zp, True, True))
-            out.append(op("v", lambda: V.tensor_tensor(T.hw[:, HW * b + col:HW * b + col + m_cols], bank(b0 + b, m_cols, at),
-                                                       T.xt[:, 4 * col + b:4 * (col + m_cols):4], A.add), [m], join=out[0] if whole and out else None))
-        free[b0] = [out[-1]]
+            to, src = T.hw[:, HW * b + col:HW * b + col + wide], bank(b0 + b, wide, skip)
+            if b in copied:
+                out[b] = op("s", lambda: S.activation(to, src, ACT.Copy), [m])
+            else:
+                out[b] = op("v", lambda: V.tensor_tensor(to, src, xt(col, col + wide, b), A.add), [m])
+        free[b0] = list(out.values())
         return out
 
     n14 = slice(0, 14)
-    own = (T.x2q[:, FAR - 128:FAR], T.x2p[:, FAR - 128:FAR], 128, PAD)
+    ev = {}
+
+    def way_home():
+        e2 = op("v", lambda: V.tensor_tensor_scan(T.tw2[:, 32:32 + SEG], T.ee[:, 0:SEG], T.hb[:], 0.0, A.mult, A.max), [c_d, f2])
+        e = op("v", lambda: V.tensor_copy(T.d0[:, n14], T.sl[:, n14]))
+        op("v", lambda: V.tensor_scalar(T.d5[:, n14], T.dc[:, n14], T.pcT[:, 0:1], None, A.add), join=e)
+        yield None
+        sw = swap(T.tw2, T.tu2, T.d1[:], e2)
+        next(sw)
+        e = op("v", lambda: V.tensor_scalar(T.d2[:, n14], T.d0[:, n14], LANE - 1, None, A.bitwise_and), on=e)
+        yield None
+        next(sw)
+        e = op("v", lambda: V.tensor_scalar(T.d4[:, n14], T.d2[:, n14], 16.0 + C, 1024.0, A.is_ge, A.mult), on=e)
+        yield None
+        e2 = next(sw)
+        e = op("v", lambda: V.tensor_tensor(T.d6[:, n14], T.d4[:, n14], T.d2[:, n14], A.add), on=e)
+        yield None
+        e2 = op("v", lambda: V.tensor_scalar(T.d3[:, n14], T.d1[:, n14], 511, None, A.bitwise_and), on=e2)
+        yield None
+        e = op("v", lambda: V.tensor_tensor(T.d7[:, n14], T.d6[:, n14], T.d3[:, n14], A.add), [e2], on=e)
+        yield None
+        e = op("v", lambda: V.tensor_tensor(T.d8[:, n14], T.d7[:, n14], T.d5[:, n14], A.min), on=e)
+        yield None
+        ev["hl"] = op("v", lambda: V.tensor_scalar(T.hl[:, n14], T.d8[:, n14], -16.0, None, A.add), on=e)
+        yield None
+
+    own = (T.x2q[:, NEAR - 128:NEAR], T.x2p[:, NEAR - 128:NEAR], 128, PAD)
     wait("t", l_a)
     wait("t", q_own)
-    e = op("v", lambda: V.tensor_copy(T.d0[:, n14], T.sl[:, n14]))
-    op("v", lambda: V.tensor_scalar(T.d5[:, n14], T.dc[:, n14], T.pcT[:, 96:97], None, A.add), [c_d], join=e)
-    e = op("v", lambda: V.tensor_scalar(T.d1[:, n14], T.d0[:, n14], 8, 7, A.logical_shift_right, A.bitwise_and), on=e)
-    op("v", lambda: V.tensor_scalar(T.d2[:, n14], T.d0[:, n14], RUN - 1, None, A.bitwise_and), join=e)
-    layer_a(0, 0, 0, *own, BY[0])
-    e = op("v", lambda: V.tensor_scalar(T.d3[:, n14], T.d1[:, n14], float(C), -16.0, A.mult, A.add), on=e)
-    op("v", lambda: V.tensor_scalar(T.d4[:, n14], T.d2[:, n14], 16.0 + C, 1024.0, A.is_ge, A.mult), join=e)
-    layer_a(0, 1, 4, *own, BY[1])
-    e = op("v", lambda: V.tensor_tensor(T.d6[:, n14], T.d3[:, n14], T.d2[:, n14], A.add), on=e)
-    e = op("v", lambda: V.tensor_tensor(T.d7[:, n14], T.d6[:, n14], T.d4[:, n14], A.add), on=e)
-    e = op("v", lambda: V.tensor_tensor(T.d8[:, n14], T.d7[:, n14], T.d5[:, n14], A.min), on=e)
-    layer_c(0, 0, 0, 128)
-    q_z0 = layer_c(0, 1, 0, 128, PAD, T.z0q[:], T.z0p[:], BY[2])
-    e_hl = op("v", lambda: V.tensor_copy(T.hl[:, n14], T.d8[:, n14]), on=e)
-
-    far, near = (T.x1lq[:], T.x1lp[:], FAR, 0), (T.x2lq[:], T.x2lp[:], NEAR, 0)
-    PE.wait_ge(T.sem.xfar, far_count)
-    m = layer_a(1, 0, 4, *far, BY[3])
-    l_v = op("q", lambda: Q.dma_start(T.vs[:], T.v[:]), [m], inc=16)
-    layer_a(1, 1, 0, *far, BY[4])
-    PE.wait_ge(T.sem.xnear, near_count)
-    layer_a(2, 0, 4, *near, BY[5])
-    layer_c(1, 0, 0, FAR)
-    send_far("z", layer_c(1, 1, 0, FAR, 0, T.z1q[:], T.z1p[:], BY[6]))
-    layer_a(2, 1, 4, *near, BY[7])
-    layer_c(2, 0, 0, NEAR)
-    send_near("z", layer_c(2, 1, 0, NEAR, 0, T.z2q[:], T.z2p[:], BY[8]))
+    layer_a(0, 0, 0, *own, by_stage[0])
+    layer_a(0, 1, 4, *own, by_stage[1])
     q_e = None
     for b in range(4):
         q_e = op("v", lambda: V.quantize_mx(T.eq[:, 128 * b:128 * b + 128], T.ep[:, 128 * b:128 * b + 128], T.eb[:, 3 - b:515 - b]), [c_e], join=q_e)
 
-    wait("t", q_e)
-    wait("t", q_z0)
-    s_own = home(4, T.z0q[:], T.z0p[:], 128, 128 - C, C, 7 * C, True)[0]
-    q_v = op("v", lambda: V.quantize_mx(T.vq[:], T.vp[:], T.vs[:]), [l_v])
-    e = op("s", lambda: S.activation(T.olb[:], T.tab[:, 0:HW].indirect(T.hl[:, n14]), ACT.Copy), [e_hl, c_tab])
-    stores = op("q", lambda: Q.dma_start(T.ol[:], T.olb[0:128:16, :]), [e], inc=16)
+    tiles = {1: (T.xlq[:, 0:FAR], T.xlp[:, 0:FAR], FAR, 0), 2: (T.xlq[:, FAR:ALL], T.xlp[:, FAR:ALL], NEAR, 0)}
+    nby, l_v = 3, None
+    for item in ORDER.split():
+        s, kind, i, b0 = int(item[0]), item[1], int(item[2]), int(item[4])
+        if kind == "a":
+            if i == 0:
+                PE.wait_ge(T.sem.xfar if s == 1 else T.sem.xnear, arriving["far" if s == 1 else "x"])
+            m = layer_a(s, i, b0, *tiles[s], by_stage[nby])
+            nby += 1
+            if l_v is None:
+                l_v = op("q", lambda: Q.dma_start(T.vs[:], T.v[:]), [m], inc=16)
+        elif i == 0:
+            layer_c(s, 0, b0, tiles[s][2])
+        elif s == 1:
+            send_far("z", layer_c(1, 1, b0, FAR, 0, T.z1q[:], T.z1p[:], by_stage[nby]))
+            nby += 1
+        else:
+            send_near("z", layer_c(2, 1, b0, NEAR, 0, T.z2q[:], T.z2p[:], by_stage[nby]))
+            nby += 1
 
-    PE.wait_ge(T.sem.zfar, far_count)
-    s_first = home(0, T.z1lq[:], T.z1lp[:], FAR, 0, FAR, 0, True)[0]
-    PE.wait_ge(T.sem.znear, near_count)
-    s_last = home(4, T.z2lq[:], T.z2lp[:], NEAR, 0, NEAR, FAR, False)
-    gs = None
-    for b, k in ((0, 14), (1, 14), (2, 8)):
-        gs = op("s", lambda: S.activation(T.yt[:, b:64 * k:4], T.hw[:, HW * b:HW * (b + 1)].indirect(T.hl[:, 0:k]), ACT.Copy),
-                [h_x, s_own, s_first, s_last[b]], join=gs)
-    gv = op("v", lambda: V.tensor_copy(T.yt[:, 512 + 2:4 * TC:4], T.hw[:, HW * 2:HW * 3].indirect(T.hl[:, 8:14])), [h_x, s_own, s_first, e_hl, s_last[2]])
-    op("v", lambda: V.tensor_copy(T.yt[:, 3:4 * TC:4], T.hw[:, HW * 3:HW * 4].indirect(T.hl[:, n14])), [s_last[3]], join=gv)
+    wh = way_home()
+    layer_c(0, 0, 4, 128)
+    next(wh)
+    q_z0 = layer_c(0, 1, 4, 128, PAD, T.z0q[:], T.z0p[:], by_stage[2])
+    for b in range(7):
+        next(wh)
+        if b == 4:
+            wait("t", q_e)
+            wait("t", q_z0)
+            s_own = home(4, T.z0q[:], T.z0p[:], 128, PAD, ALL)
+        if b == 5:
+            q_v = op("v", lambda: V.quantize_mx(T.vq[:], T.vp[:], T.vs[:]), [l_v])
+    e_hl = ev["hl"]
+
+    outs = []
+    for k, s in enumerate(HOME):
+        if s == "1":
+            PE.wait_ge(T.sem.zfar, arriving["far"])
+            outs.append(home(4 * k, T.zlq[:, 0:FAR], T.zlp[:, 0:FAR], FAR, 0, 0))
+        else:
+            PE.wait_ge(T.sem.znear, arriving["z"])
+            outs.append(home(4 * k, T.zlq[:, FAR:ALL], T.zlp[:, FAR:ALL], NEAR, 0, FAR))
+    gs = gv = None
+    for b in range(4):
+        need = [h_x, e_hl, s_own[b], outs[0][b], outs[1][b]]
+        out, src = T.yt[:, b:4 * TC:4], T.hw[:, HW * b:HW * (b + 1)].indirect(T.hl[:, n14])
+        if b in copied:
+            gv = op("v", lambda: V.tensor_tensor(out, src, T.xpl[:, TC * b:TC * (b + 1)], A.add), need, join=gv)
+        else:
+            gs = op("s", lambda: S.activation(out, src, ACT.Copy), need, join=gs)
     q_y = op("v", lambda: V.quantize_mx(T.yq[:], T.yp[:], T.yt[:]), [gs], on=gv)
+    e_ol = op("s", lambda: S.activation(T.olb[:], T.tab[:, 0:HW].indirect(T.hl[:, n14]), ACT.Copy), [c_tab])
     take(0)
-    m = op("t", lambda: PE.matmul_mx(bank(0, TC), T.vq[:], T.vp[:], T.yq[:], T.yp[:], True, True), [q_v, q_y])
-    op("q", lambda: Q.dma_start(T.oc[:], _u8(T.yq[:])), [q_y], join=stores, inc=16)
+    m0 = op("t", lambda: PE.matmul_mx(bank(0, 128), T.vq[:], T.vp[:], T.yq[:, 0:128], T.yp[:, 0:128], True, True), [q_v, q_y])
+    m1 = op("t", lambda: PE.matmul_mx(bank(1, 128), T.vq[:], T.vp[:], T.yq[:, TC - 128:TC], T.yp[:, TC - 128:TC], True, True))
+    stores = op("q", lambda: Q.dma_start(T.oc[:], _u8(T.yq[:])), [q_y], inc=16)
     for k in range(4):
-        q = "qqss"[k]
-        op(q, lambda: queues[q].dma_start(T.osc[4 * k:4 * k + 4, :], T.yp[32 * k:32 * k + 4, :]), [q_y], join=stores, inc=16)
-    e = op("v", lambda: V.tensor_copy(T.yo[:], bank(0, TC)), [m])
-    op("s", lambda: S.dma_start(T.y[:], T.yo[:]), [e], join=stores, inc=16)
+        op("q", lambda: Q.dma_start(T.osc[4 * k:4 * k + 4, :], T.yp[32 * k:32 * k + 4, :]), join=stores, inc=16)
+    op("q", lambda: Q.dma_start(T.ol[:], T.olb[0:128:16, :]), [e_ol], join=stores, inc=16)
+    e = op("s", lambda: S.activation(T.yo[:, 0:128], bank(0, 128), ACT.Copy), [m0])
+    e1 = op("v", lambda: V.tensor_copy(T.yo[:, 128:TC], bank(1, TC - 128, 256 - TC)), [m1])
+    op("s", lambda: S.dma_start(T.y[:], T.yo[:]), [e, e1], join=stores, inc=16)
     g.wait_ge(T.sem.sent, sent[0])
     for name in top:
         if max([seen.get((q, name), 0) for q in queues]) < top[name]:

from concourse.bass import DstId, RemoteDMATransfer
from concourse.mybir import dt, AluOpType, ActivationFunctionType

N, TC, C = 8, 224, 48
FAR, NEAR, ALL = 4 * C, 3 * C, 7 * C
PAD = 128 - C
SEG = TC // 2
LANE = 256
HW = 8 * C + TC
F8, U8, U16, BF, F32, I32 = "float8_e4m3fn_x4", "uint8", "uint16", "bfloat16", "float32", "int32"
BIG = 1e29
ORDER = "2a0:4 2a1:0 1a0:4 1a1:0 1c0:4 1c1:4 2c0:0 2c1:0"
BY = "svsv sssv svsv svsv sssv svsv sssv svsv svsv"
HOME = "21"


def _sb(n, d):
    return ("sbuf", [128, n], d)


SCRATCH = {
    "ps": ("psum", [128, 4096], F32),
    "xs": _sb(4 * TC, BF), "us": _sb(512, BF), "vs": _sb(512, BF),
    "xq": _sb(256, F8), "xp": _sb(256, U8), "uq": _sb(128, F8), "up": _sb(128, U8),
    "uq2": _sb(128, F8), "up2": _sb(128, U8), "vq": _sb(128, F8), "vp": _sb(128, U8),
    "aq": _sb(1024, F8), "apl": _sb(1024, U8), "cq": _sb(1024, F8), "cpl": _sb(1024, U8),
    "pidx": _sb(8, I32), "i16": _sb(8, I32), "t0": _sb(8, I32), "t1": _sb(8, I32), "uoff": _sb(8, U16),
    "pc": _sb(64, F32), "pcT": _sb(64, F32), "glist": _sb(2, U16), "crT": _sb(TC, BF),
    "jv": _sb(TC, BF), "pf": _sb(64, F32), "pb": _sb(64, F32), "crow": _sb(TC, BF), "im": _sb(C, BF), "diag": _sb(C, BF),
    "pt": _sb(TC, F32), "rf": _sb(SEG, F32), "rb": _sb(128, F32), "ee": _sb(SEG + 8, BF), "gs": _sb(TC, BF), "gT": _sb(TC, BF),
    "val": _sb(TC, BF), "vT": _sb(TC, BF), "mm": _sb(SEG, F32), "tw": _sb(32 + 512, F32), "tu": _sb(64, F32), "sl": _sb(16, U16),
    "hb": _sb(SEG, F32), "tw2": _sb(32 + 512, F32), "tu2": _sb(64, F32),
    "win": _sb(N * LANE, BF), "ex": _sb(N * C, BF), "il": _sb(32, U16),
    "xpl": _sb(4 * TC, BF), "xt": _sb(4 * (PAD + N * C), BF),
    "x0q": _sb(128, F8), "x0p": _sb(128, U8), "x1q": _sb(FAR, F8), "x1p": _sb(FAR, U8), "x2q": _sb(NEAR, F8), "x2p": _sb(NEAR, U8),
    "xlq": _sb(ALL, F8), "xlp": _sb(ALL, U8),
    "z0q": _sb(128, F8), "z0p": _sb(128, U8), "z1q": _sb(FAR, F8), "z1p": _sb(FAR, U8), "z2q": _sb(NEAR, F8), "z2p": _sb(NEAR, U8),
    "zlq": _sb(ALL, F8), "zlp": _sb(ALL, U8),
    "rxq": _sb(2 * C, F8), "rxp": _sb(2 * C, U8), "rzq": _sb(2 * C, F8), "rzp": _sb(2 * C, U8),
    "ht": _sb(24 * FAR, BF), "hq": _sb(6 * FAR, F8), "hp": _sb(6 * FAR, U8), "zt": _sb(12 * FAR, BF),
    "eb": _sb(516, BF), "eq": _sb(512, F8), "ep": _sb(512, U8),
    "hw": _sb(4 * HW, BF), "tab": _sb(HW, F32), "olb": _sb(TC, F32),
    "d0": _sb(16, I32), "d1": _sb(16, I32), "d2": _sb(16, I32), "d3": _sb(16, I32), "d4": _sb(16, F32),
    "d5": _sb(16, F32), "d6": _sb(16, F32), "d7": _sb(16, F32), "d8": _sb(16, F32), "dc": _sb(16, F32), "hl": _sb(16, U16),
    "yt": _sb(4 * TC, BF), "yq": _sb(TC, F8), "yp": _sb(TC, U8), "yo": _sb(TC, F32),
}
SEMAPHORES = ["sent", "xfar", "xnear", "zfar", "znear", "rx", "rz"] + ["e%d" % k for k in range(143)]


def _mask(engines):
    m = 0
    for e in engines:
        m |= 1 << e
    return m


def _plan(T, topo):
    cores = T.cores
    plan = []
    for r in range(N):
        far = [d for d in range(N) if d != r and not topo.may_write(cores[r], cores[d])]
        mine = [d for d in range(N) if d not in far]
        assert len(far) == 4
        i = mine.index(r)
        far = far[i:] + far[:i]
        near = [mine[i ^ k] for k in (1, 2, 3)]
        able = [c for c in topo.cores_of(cores[r]) if c not in cores and all(topo.may_write(c, cores[d]) for d in far)]
        same = [c for c in able if topo.die(c) == topo.die(cores[r])]
        across = [c for c in able if topo.die(c) != topo.die(cores[r])]
        plan.append({"order": far + near + [r], "codes": [across[0], same[0]], "scales": [across[1], same[1]]})
    return plan


def _near_masks(topo, src, dst, stage):
    e = topo.engines(src, dst)
    a, b = e[0::2], e[1::2]
    q = len(a) // 2
    if stage == "x":
        return [e, a, b], [e, a, b]
    return [a, b[:q], b[q:]], [a[:q], a[q:], b]


def _hand_engines(topo, plan, T, r, kind, t):
    return topo.engines(T.cores[r], plan[r][kind][t])[t::2]


def _dst(topo, dst, src):
    rid, pid = topo.addr(dst, src)
    return DstId(rid=rid, pnc=pid)


def _u8(v):
    return v.bitcast(dt.uint8)


def _helper(g, core, T, topo, plan):
    for r in range(N):
        for kind in ("codes", "scales"):
            if core in plan[r][kind]:
                t = plan[r][kind].index(core)
                total = 0
                for stage in ("x", "z"):
                    g.wait_ge(T.sem["r" + stage], len(_hand_engines(topo, plan, T, r, kind, t)))
                    tr = []
                    for k in range(2):
                        d = plan[r]["order"][2 * t + k]
                        e = topo.engines(core, T.cores[d])
                        e = e[k * (len(e) // 2):(k + 1) * (len(e) // 2)]
                        at = C * plan[d]["order"].index(r)
                        if kind == "codes":
                            src, dst = _u8(T["r%sq" % stage][:, C * k:C * k + C]), _u8(T[stage + "lq"][:, at:at + C])
                        else:
                            src, dst = T["r%sp" % stage][:, C * k:C * k + C], T[stage + "lp"][:, at:at + C]
                        tr.append(RemoteDMATransfer(dst_ids=[_dst(topo, T.cores[d], core)], dma_engine_mask=_mask(e),
                                                    remote_sem=T.sem[stage + "far"], src=src, dst=dst))
                        total += len(e)
                    g.remote_dma_fused(tr, local_sem=T.sem.sent)
                g.wait_ge(T.sem.sent, total)


def rank_program(g, core, T, topo):
    plan = _plan(T, topo)
    r = T.rank_of(core)
    if r is None:
        _helper(g, core, T, topo, plan)
        return
    me = plan[r]
    order = me["order"]
    V, S, PE, Q = g.vector, g.scalar, g.tensor, g.sync
    queues = {"g": g, "v": V, "s": S, "t": PE, "q": Q}
    A, ACT = AluOpType, ActivationFunctionType
    top, seen, used = {}, {}, [0]
    by_stage = BY.split()

    def wait(q, e):
        if seen.get((q, e[0]), 0) < e[1]:
            queues[q].wait_ge(T.sem[e[0]], e[1])
            seen[(q, e[0])] = e[1]

    def op(q, call, deps=(), join=None, on=None, inc=1):
        for e in deps:
            if e:
                wait(q, e)
        if on is not None:
            wait(q, on)
            assert top[on[0]] == on[1]
            e = [on[0], on[1]]
        elif join is not None:
            e = join
        else:
            e = ["e%d" % used[0], 0]
            used[0] += 1
        call().then_inc(T.sem[e[0]], inc)
        e[1] += inc
        top[e[0]] = e[1]
        return e

    def bank(k, n, at=0):
        return T.ps[:, 512 * k + at:512 * k + at + n]

    def iota(out, pattern, base, cm=0, join=None, deps=()):
        if out.dtype == T.pidx.dtype:
            return op("g", lambda: g.iota(out, pattern, base, cm), deps, join=join)
        return op("g", lambda: g.iota(out, pattern, base, cm, allow_small_or_imprecise_dtypes=True), deps, join=join)

    def fill(view, value, join=None):
        return op("v", lambda: V.memset(view, value), join=join)

    def run(d):
        return LANE * (N - 1 - d) + 16

    def xt(c0, c1, b=None):
        lo, hi = (4 * c0, 4 * c1) if c0 < FAR else (4 * (PAD + c0), 4 * (PAD + c1))
        return T.xt[:, lo:hi] if b is None else T.xt[:, lo + b:hi:4]

    l_u = op("q", lambda: Q.dma_start(T.us[:], T.u[:]), inc=16)
    l_xa = op("q", lambda: Q.dma_start(T.xs[:, 0:512], T.x[:, 0:512]), inc=16)
    l_xb = op("q", lambda: Q.dma_start(T.xs[:, 512:4 * TC], T.x[:, 512:4 * TC]), inc=16)
    l_a = op("q", lambda: Q.dma_start(_u8(T.aq[:]), T.ac[:]), inc=16)
    op("q", lambda: Q.dma_start(T.apl[:], T.ap[:]), join=l_a, inc=16)
    l_c = op("q", lambda: Q.dma_start(_u8(T.cq[:]), T.cc[:]), inc=16)
    op("q", lambda: Q.dma_start(T.cpl[:], T.cp[:]), join=l_c, inc=16)

    c_p = iota(T.pidx[:], [[0, 8]], 0, 1)
    iota(T.i16[:], [[16, 8]], 0, join=c_p)
    c_pc = iota(T.pc[:, 0:32], [[0, 2], [1, 16]], 0)
    for h in range(2):
        for par in range(2):
            view = T.pc[:, 32 + 16 * h + par:48 + 16 * h:2]
            iota(view, [[16, 8]], 32 + 8 * h + 7, join=c_pc) if par == h else iota(view, [[1, 8]], 0, join=c_pc)
    c_j = iota(T.jv[:], [[1, TC]], 0)
    iota(T.im[:], [[0, 3], [1, 16]], 0, join=c_j)
    c_w = None
    for d in order:
        c_w = iota(T.win[:, run(d):run(d) + C], [[0, C]], TC - 1, join=c_w)

    m0 = fill(T.pf[:], 0.0)
    fill(T.pb[:], 0.0, m0)
    fill(T.crT[:], 0.0, m0)
    c_e = fill(T.eb[:], 1.0)
    m2 = op("v", lambda: V.memset(T.crT[:, 2 * (N - 1):TC:16], 1.0), [m0])
    e = op("v", lambda: V.tensor_scalar(T.t0[:], T.pidx[:], 1, 7, A.logical_shift_right, A.bitwise_and), [c_p])
    m1 = fill(T.rb[:, 64:128:56], BIG)
    fill(T.ee[:, 0:1], 0.0, m1)
    e = op("v", lambda: V.tensor_tensor(T.t1[:], T.t0[:], T.i16[:], A.add), on=e)
    fill(T.gs[:, 1:TC:2], 0.0, m1)
    fill(T.tw[:, 32 + SEG + 7:544:8], 0.0, m1)
    c_uo = op("v", lambda: V.tensor_copy(T.uoff[:], T.t1[:]), on=e)
    fill(T.pf[:, 0:64:8], -BIG, m1)
    fill(T.pb[:, 0:64:8], -9 * BIG, m1)
    fill(T.pb[:, 7:64:8], BIG, m1)
    op("v", lambda: V.transpose(T.crow[:], T.crT[:]), [m2], join=m1)
    c_e = op("g", lambda: g.affine_select(T.eb[:], T.eb[:], [[1, 516]], A.is_equal, 0.0, -3, -4), [c_e])

    q_u = op("v", lambda: V.quantize_mx(T.uq[:], T.up[:], T.us[:]), [l_u])
    f2 = fill(T.tw2[:, 32 + SEG + 7:544:8], 0.0)
    k_u = op("v", lambda: V.tensor_copy(T.uq2[:, 0:128].bitcast(dt.uint32), T.uq[:, 0:128].bitcast(dt.uint32).indirect(T.uoff[:, 0:8])), [q_u, c_uo])
    k_s = op("s", lambda: S.activation(T.up2[:, 0:128], T.up[:, 0:128].indirect(T.uoff[:, 0:8]), ACT.Copy), [q_u, c_uo])
    q_xa = op("v", lambda: V.quantize_mx(T.xq[:, 0:128], T.xp[:, 0:128], T.xs[:, 0:512]), [l_xa])
    m_a = op("t", lambda: PE.matmul_mx(bank(0, 128), T.uq2[:], T.up2[:], T.xq[:, 0:128], T.xp[:, 0:128], True, True), [k_u, k_s, q_xa])
    q_xb = op("v", lambda: V.quantize_mx(T.xq[:, 128:256], T.xp[:, 128:256], T.xs[:, 4 * TC - 512:4 * TC]), [l_xb])
    m_b = op("t", lambda: PE.matmul_mx(bank(1, 128), T.uq2[:], T.up2[:], T.xq[:, 128:256], T.xp[:, 128:256], True, True), [q_xb])
    pl = None
    for t in range(4):
        pl = op("s", lambda: S.activation(T.xpl[:, TC * t:TC * t + TC], T.xs[:, t:4 * TC:4], ACT.Copy), [l_xa, l_xb], join=pl)

    cols, segs, wins = ((0, 128), (128, TC)), ((0, 64), (64, SEG)), (0, 72)
    lanes = {}

    def back(buf, lo, hi, st):
        last = lo + (hi - lo - 1) // st * st
        return buf[:, last::-st] if lo < st else buf[:, last:lo - st:-st]

    def step(k, h, deps=(), on=None):
        (c0, c1), (s0, s1), w = cols[h], segs[h], wins[h]
        n = s1 - s0
        if k == 0:
            return op("v", lambda: V.transpose(T.pt[:, c0:c1], bank(h, c1 - c0, 128 - (c1 - c0))), deps, on=on)
        if k == 1:
            e = op("v", lambda: V.tensor_tensor_scan(T.rf[:, s0:s1], T.pf[:, 0:n], T.pt[:, c0:c1:2], 0.0, A.add, A.max), deps, on=on)
            return op("v", lambda: V.tensor_tensor_scan(back(T.rb, w, w + n, 1), T.pb[:, 0:n], back(T.pt, c0, c1, 2), 0.0, A.add, A.max), join=e)
        if k == 2:
            return op("v", lambda: V.tensor_tensor(T.ee[:, s0 + 1:s1 + 1], T.rf[:, s0:s1], T.rb[:, w + 1:w + 1 + n], A.is_ge), deps, on=on)
        if k == 3:
            lanes[h] = op("s", lambda: S.activation(T.mm[:, s0:s1], T.ee[:, s0:s1], ACT.Identity, scale=4096.0 + LANE, bias=-4096.0), [on])
            return op("v", lambda: V.tensor_tensor(T.gs[:, c0:c1:2], T.ee[:, s0 + 1:s1 + 1], T.ee[:, s0:s1], A.subtract), deps, on=on)
        if k == 4:
            return op("v", lambda: V.transpose(T.gT[:, c0:c1], T.gs[:, c0:c1]), deps, on=on)
        if k == 5:
            first = T.val[:, c0 - 1:c0] if h else 15.0
            return op("v", lambda: V.tensor_tensor_scan(T.val[:, c0:c1], T.crow[:, c0:c1], T.gT[:, c0:c1], first, A.add, A.add), deps, on=on)
        if k == 6:
            return op("v", lambda: V.transpose(T.vT[:, c0:c1], T.val[:, c0:c1]), deps, on=on)
        return op("v", lambda: V.tensor_tensor_scan(T.tw[:, 32 + s0:32 + s1], T.mm[:, s0:s1], T.vT[:, c0:c1:2], 0.0, A.add, A.max), [lanes[h]], on=on)

    def swap(tw, tu, out, e, deps=()):
        e = op("v", lambda: V.transpose(tu[:, 0:32], tw[:, 39:544:16]), on=e)
        op("v", lambda: V.transpose(tu[:, 32:64], tw[:, 47:544:16]), join=e)
        yield None
        e = op("v", lambda: V.transpose(tw[:, 0:32], tu[:, 16:48]), on=e)
        yield None
        yield op("v", lambda: V.tensor_scalar(out, tw[:, 0:32 + SEG].indirect(T.glist[:, 0:1]), 0.0, None, A.add), deps, on=e)

    ea = step(0, 0, [m_a, m1])
    ea = step(1, 0, on=ea)
    eb = step(0, 1, [m_b])
    for k in range(2, 8):
        ea = step(k, 0, on=ea)
        eb = step(k - 1, 1, on=eb)
        if k == 4:
            c_t = op("v", lambda: V.transpose(T.pcT[:], T.pc[:]), [c_pc])
        if k == 6:
            c_l = op("v", lambda: V.tensor_scalar(T.glist[:], T.pcT[:, 32:34], 31.0 + SEG, None, A.min), [c_t])
        if k == 7:
            op("v", lambda: V.tensor_scalar(T.diag[:], T.im[:], T.pcT[:, 0:1], 512.0, A.is_equal, A.mult), [c_j], join=c_l)
    e = step(7, 1, on=eb)
    wait("v", ea)
    e_sl = list(swap(T.tw, T.tu, T.sl[:], e, [c_l]))[-1]
    e_sc = op("v", lambda: V.tensor_copy(T.win[:, 0:N * LANE].indirect(T.sl[:, 0:14]), T.jv[:]), [c_w, e_sl])

    copied = (2, 3)
    pad = None
    for tile in (T.xt[:, 4 * FAR:4 * (FAR + PAD)], T.ht[:, 0:4 * PAD], T.ht[:, 4 * FAR:4 * (FAR + PAD)], T.zt[:, 0:4 * PAD]):
        pad = op("s", lambda: S.activation(tile, T.xs[:, 0:4 * PAD], ACT.Identity, scale=0.0), join=pad)
    h_x = None
    for t in range(4):
        if t in copied:
            h_x = op("s", lambda: S.activation(T.hw[:, HW * t + N * C:HW * (t + 1)], T.xs[:, 0:TC], ACT.Identity, scale=0.0), join=h_x)
        else:
            h_x = op("s", lambda: S.activation(T.hw[:, HW * t + N * C:HW * (t + 1)], T.xs[:, t:4 * TC:4], ACT.Copy), join=h_x)

    sent = [0]

    def send_far(stage, dep):
        wait("g", dep)
        for kind in ("codes", "scales"):
            tr = []
            for t in range(2):
                eng = _hand_engines(topo, plan, T, r, kind, t)
                if kind == "codes":
                    src, dst = _u8(T[stage + "1q"][:, 2 * C * t:2 * C * (t + 1)]), _u8(T["r%sq" % stage][:])
                else:
                    src, dst = T[stage + "1p"][:, 2 * C * t:2 * C * (t + 1)], T["r%sp" % stage][:]
                tr.append(RemoteDMATransfer(dst_ids=[_dst(topo, me[kind][t], core)], dma_engine_mask=_mask(eng), remote_sem=T.sem["r" + stage], src=src, dst=dst))
                sent[0] += len(eng)
            g.remote_dma_fused(tr, local_sem=T.sem.sent)

    def send_near(stage, dep, ks=(0, 1, 2), kinds=(0, 1), buf="2", at=0):
        if dep:
            wait("g", dep)
        for kind in kinds:
            tr = []
            for k in ks:
                d = order[4 + k]
                eng = _near_masks(topo, core, T.cores[d], stage)[kind][k]
                a = at + C * (k - ks[0])
                b = C * plan[d]["order"].index(r)
                if kind == 0:
                    src, dst = _u8(T[stage + buf + "q"][:, a:a + C]), _u8(T[stage + "lq"][:, b:b + C])
                else:
                    src, dst = T[stage + buf + "p"][:, a:a + C], T[stage + "lp"][:, b:b + C]
                tr.append(RemoteDMATransfer(dst_ids=[_dst(topo, T.cores[d], core)], dma_engine_mask=_mask(eng), remote_sem=T.sem[stage + "near"], src=src, dst=dst))
                sent[0] += len(eng)
            g.remote_dma_fused(tr, local_sem=T.sem.sent)

    arriving = {"far": sum(2 * (len(topo.engines(plan[s]["codes"][0], core)) // 2) for s in order[:4])}
    for stage in ("x", "z"):
        arriving[stage] = sum(len(_near_masks(topo, T.cores[s], core, stage)[kind][plan[s]["order"].index(r) - 4]) for s in order[4:7] for kind in range(2))

    sets, at_il = [(4, 5), (0, 4), (5, 8), (0, 2), (2, 4)], [0, 4, 16, 4, 10]

    def pick(b, join=None):
        w = run(order[b])
        return op("v", lambda: V.tensor_tensor_scan(T.ex[:, C * b:C * b + C], T.diag[:], T.win[:, w:w + C], 0.0, A.add, A.min), [e_sc], join=join)

    def listed(s, e):
        b0, b1 = sets[s]
        return op("v", lambda: V.tensor_copy(T.il[:, at_il[s]:at_il[s] + 3 * (b1 - b0)], T.ex[:, C * b0 + 15:C * b1:16]), on=e)

    def gather(q, s, ts, e, join=None):
        b0, b1 = sets[s]
        for t in ts:
            out, src = xt(C * b0, C * b1, t), T.xpl[:, TC * t:TC * (t + 1)].indirect(T.il[:, at_il[s]:at_il[s] + 3 * (b1 - b0)])
            if q == "s":
                join = op("s", lambda: S.activation(out, src, ACT.Copy), [e, pl], join=join)
            else:
                join = op("v", lambda: V.tensor_copy(out, src), [e, pl], join=join)
        return join

    e1 = pick(4)
    ef = pick(1, pick(0))
    e1 = listed(0, e1)
    ef = pick(3, pick(2, ef))
    gv = gather("v", 0, (0,), e1)
    gs = gather("s", 0, (2, 3), e1)
    ef = listed(1, ef)
    gv = gather("v", 0, (1,), e1, gv)
    en = pick(6, pick(5))
    send_near("x", op("v", lambda: V.quantize_mx(T.x0q[:], T.x0p[:], T.xt[:, 4 * FAR:4 * (FAR + 128)]), [gs, pad], on=gv), (0,), (0,), "0", PAD)
    gs = gather("s", 4, (1,), ef, gather("s", 1, (2, 3), ef))
    gv = gather("v", 1, (0,), ef)
    en = pick(7, en)
    gv = gather("v", 3, (1,), ef, gv)
    en = listed(2, en)
    send_far("x", op("v", lambda: V.quantize_mx(T.x1q[:], T.x1p[:], xt(0, FAR)), [gs], on=gv))
    send_near("x", None, (0,), (1,), "0", PAD)
    gs = gather("s", 2, (2, 3), en)
    gv = gather("v", 2, (0, 1), en)
    q_own = op("v", lambda: V.quantize_mx(T.x2q[:], T.x2p[:], xt(FAR + C, N * C)), [gs], on=gv)
    send_near("x", q_own, (1, 2))

    c_d = iota(T.dc[:], [[16, 16]], N * C + 16)
    for d in range(N):
        iota(T.hb[:, d:SEG:8], [[0, SEG // 8]], 512 * (N - 1 - d) + C * order.index(d), join=c_d)
    c_tab = None
    for pos in range(N):
        c_tab = iota(T.tab[:, C * pos:C * pos + C], [[1, C]], C * order[pos], join=c_tab)
    iota(T.tab[:, N * C:HW], [[0, TC]], -1, join=c_tab)

    def evacuate(q, out, src, relu, dep, on):
        if q == "s":
            return op("s", lambda: S.activation(out, src, ACT.Relu if relu else ACT.Identity, scale=0.0625), [dep], join=on)
        if relu:
            return op("v", lambda: V.tensor_scalar(out, src, 0.0, 0.0625, A.max, A.mult), [dep], join=on)
        return op("v", lambda: V.tensor_scalar(out, src, 0.0625, None, A.mult), [dep], join=on)

    free = {0: [], 4: []}

    def take(b0):
        for e in free[b0]:
            wait("t", e)

    q_h = {}

    def layer_a(s, i, b0, xc, xp, n, skip, by):
        take(b0)
        k = 2 * s + i
        lo = 4 * FAR * k
        done = {"s": None, "v": None}
        for b in range(4):
            w = 512 * i + 128 * b
            m = op("t", lambda: PE.matmul_mx(bank(b0 + b, n), T.aq[:, w:w + 128], T.apl[:, w:w + 128], xc, xp, True, True))
            done[by[b]] = evacuate(by[b], T.ht[:, lo + 4 * skip + b:lo + 4 * n:4], bank(b0 + b, n - skip, skip), True, m, done[by[b]])
        free[b0] = [list(e) for e in done.values() if e]
        q_h[k] = op("v", lambda: V.quantize_mx(T.hq[:, FAR * k:FAR * k + n], T.hp[:, FAR * k:FAR * k + n], T.ht[:, lo:lo + 4 * n]),
                    [done["s"]], on=done["v"])
        return m

    def layer_c(s, i, b0, n, skip=0, oq=None, osc=None, by=None):
        k = 2 * s + i
        lo = 4 * FAR * s
        if i == 0:
            take(b0)
        wait("t", l_c)
        wait("t", q_h[k])
        done = {"s": None, "v": None}
        for b in range(4):
            w = 512 * i + 128 * b
            call = lambda: PE.matmul_mx(bank(b0 + b, n), T.cq[:, w:w + 128], T.cpl[:, w:w + 128],
                                        T.hq[:, FAR * k:FAR * k + n], T.hp[:, FAR * k:FAR * k + n], i == 0, i == 1)
            if i == 0:
                call()
            else:
                m = op("t", call)
                done[by[b]] = evacuate(by[b], T.zt[:, lo + 4 * skip + b:lo + 4 * n:4], bank(b0 + b, n - skip, skip), False, m, done[by[b]])
        if i == 1:
            free[b0] = [list(e) for e in done.values() if e]
            return op("v", lambda: V.quantize_mx(oq, osc, T.zt[:, lo:lo + 4 * n]), [done["s"]], on=done["v"])

    def home(b0, zc, zp, n, skip, col):
        out = {}
        take(b0)
        wide = n - skip
        for b in (2, 0, 3, 1):
            m = op("t", lambda: PE.matmul_mx(bank(b0 + b, n), T.eq[:, 128 * b:128 * b + 128], T.ep[:, 128 * b:128 * b + 128], zc, zp, True, True))
            to, src = T.hw[:, HW * b + col:HW * b + col + wide], bank(b0 + b, wide, skip)
            if b in copied:
                out[b] = op("s", lambda: S.activation(to, src, ACT.Copy), [m])
            else:
                out[b] = op("v", lambda: V.tensor_tensor(to, src, xt(col, col + wide, b), A.add), [m])
        free[b0] = list(out.values())
        return out

    n14 = slice(0, 14)
    ev = {}

    def way_home():
        e2 = op("v", lambda: V.tensor_tensor_scan(T.tw2[:, 32:32 + SEG], T.ee[:, 0:SEG], T.hb[:], 0.0, A.mult, A.max), [c_d, f2])
        e = op("v", lambda: V.tensor_copy(T.d0[:, n14], T.sl[:, n14]))
        op("v", lambda: V.tensor_scalar(T.d5[:, n14], T.dc[:, n14], T.pcT[:, 0:1], None, A.add), join=e)
        yield None
        sw = swap(T.tw2, T.tu2, T.d1[:], e2)
        next(sw)
        e = op("v", lambda: V.tensor_scalar(T.d2[:, n14], T.d0[:, n14], LANE - 1, None, A.bitwise_and), on=e)
        yield None
        next(sw)
        e = op("v", lambda: V.tensor_scalar(T.d4[:, n14], T.d2[:, n14], 16.0 + C, 1024.0, A.is_ge, A.mult), on=e)
        yield None
        e2 = next(sw)
        e = op("v", lambda: V.tensor_tensor(T.d6[:, n14], T.d4[:, n14], T.d2[:, n14], A.add), on=e)
        yield None
        e2 = op("v", lambda: V.tensor_scalar(T.d3[:, n14], T.d1[:, n14], 511, None, A.bitwise_and), on=e2)
        yield None
        e = op("v", lambda: V.tensor_tensor(T.d7[:, n14], T.d6[:, n14], T.d3[:, n14], A.add), [e2], on=e)
        yield None
        e = op("v", lambda: V.tensor_tensor(T.d8[:, n14], T.d7[:, n14], T.d5[:, n14], A.min), on=e)
        yield None
        ev["hl"] = op("v", lambda: V.tensor_scalar(T.hl[:, n14], T.d8[:, n14], -16.0, None, A.add), on=e)
        yield None

    own = (T.x2q[:, NEAR - 128:NEAR], T.x2p[:, NEAR - 128:NEAR], 128, PAD)
    wait("t", l_a)
    wait("t", q_own)
    layer_a(0, 0, 0, *own, by_stage[0])
    layer_a(0, 1, 4, *own, by_stage[1])
    q_e = None
    for b in range(4):
        q_e = op("v", lambda: V.quantize_mx(T.eq[:, 128 * b:128 * b + 128], T.ep[:, 128 * b:128 * b + 128], T.eb[:, 3 - b:515 - b]), [c_e], join=q_e)

    tiles = {1: (T.xlq[:, 0:FAR], T.xlp[:, 0:FAR], FAR, 0), 2: (T.xlq[:, FAR:ALL], T.xlp[:, FAR:ALL], NEAR, 0)}
    nby, l_v = 3, None
    for item in ORDER.split():
        s, kind, i, b0 = int(item[0]), item[1], int(item[2]), int(item[4])
        if kind == "a":
            if i == 0:
                PE.wait_ge(T.sem.xfar if s == 1 else T.sem.xnear, arriving["far" if s == 1 else "x"])
            m = layer_a(s, i, b0, *tiles[s], by_stage[nby])
            nby += 1
            if l_v is None:
                l_v = op("q", lambda: Q.dma_start(T.vs[:], T.v[:]), [m], inc=16)
        elif i == 0:
            layer_c(s, 0, b0, tiles[s][2])
        elif s == 1:
            send_far("z", layer_c(1, 1, b0, FAR, 0, T.z1q[:], T.z1p[:], by_stage[nby]))
            nby += 1
        else:
            send_near("z", layer_c(2, 1, b0, NEAR, 0, T.z2q[:], T.z2p[:], by_stage[nby]))
            nby += 1

    wh = way_home()
    layer_c(0, 0, 4, 128)
    next(wh)
    q_z0 = layer_c(0, 1, 4, 128, PAD, T.z0q[:], T.z0p[:], by_stage[2])
    for b in range(7):
        next(wh)
        if b == 4:
            wait("t", q_e)
            wait("t", q_z0)
            s_own = home(4, T.z0q[:], T.z0p[:], 128, PAD, ALL)
        if b == 5:
            q_v = op("v", lambda: V.quantize_mx(T.vq[:], T.vp[:], T.vs[:]), [l_v])
    e_hl = ev["hl"]

    outs = []
    for k, s in enumerate(HOME):
        if s == "1":
            PE.wait_ge(T.sem.zfar, arriving["far"])
            outs.append(home(4 * k, T.zlq[:, 0:FAR], T.zlp[:, 0:FAR], FAR, 0, 0))
        else:
            PE.wait_ge(T.sem.znear, arriving["z"])
            outs.append(home(4 * k, T.zlq[:, FAR:ALL], T.zlp[:, FAR:ALL], NEAR, 0, FAR))
    gs = gv = None
    for b in range(4):
        need = [h_x, e_hl, s_own[b], outs[0][b], outs[1][b]]
        out, src = T.yt[:, b:4 * TC:4], T.hw[:, HW * b:HW * (b + 1)].indirect(T.hl[:, n14])
        if b in copied:
            gv = op("v", lambda: V.tensor_tensor(out, src, T.xpl[:, TC * b:TC * (b + 1)], A.add), need, join=gv)
        else:
            gs = op("s", lambda: S.activation(out, src, ACT.Copy), need, join=gs)
    q_y = op("v", lambda: V.quantize_mx(T.yq[:], T.yp[:], T.yt[:]), [gs], on=gv)
    e_ol = op("s", lambda: S.activation(T.olb[:], T.tab[:, 0:HW].indirect(T.hl[:, n14]), ACT.Copy), [c_tab])
    take(0)
    m0 = op("t", lambda: PE.matmul_mx(bank(0, 128), T.vq[:], T.vp[:], T.yq[:, 0:128], T.yp[:, 0:128], True, True), [q_v, q_y])
    m1 = op("t", lambda: PE.matmul_mx(bank(1, 128), T.vq[:], T.vp[:], T.yq[:, TC - 128:TC], T.yp[:, TC - 128:TC], True, True))
    stores = op("q", lambda: Q.dma_start(T.oc[:], _u8(T.yq[:])), [q_y], inc=16)
    for k in range(4):
        op("q", lambda: Q.dma_start(T.osc[4 * k:4 * k + 4, :], T.yp[32 * k:32 * k + 4, :]), join=stores, inc=16)
    op("q", lambda: Q.dma_start(T.ol[:], T.olb[0:128:16, :]), [e_ol], join=stores, inc=16)
    e = op("s", lambda: S.activation(T.yo[:, 0:128], bank(0, 128), ACT.Copy), [m0])
    e1 = op("v", lambda: V.tensor_copy(T.yo[:, 128:TC], bank(1, TC - 128, 256 - TC)), [m1])
    op("s", lambda: S.dma_start(T.y[:], T.yo[:]), [e, e1], join=stores, inc=16)
    g.wait_ge(T.sem.sent, sent[0])
    for name in top:
        if max([seen.get((q, name), 0) for q in queues]) < top[name]:
            wait("g", [name, top[name]])
